import numpy as np, ml_dtypes
CORES = [35,38,43,46]
N = 4
BF = ml_dtypes.bfloat16
def gentries(a):
    return np.ascontiguousarray(a.reshape(8, 16, -1).transpose(0, 2, 1)).reshape(8, -1)
def gtable(e):
    e = np.asarray(e); return np.ascontiguousarray(e.reshape(8, -1, 16).transpose(0, 2, 1)).reshape(128, -1).astype(np.int32)
V, C, S, RO = 4096, 1024, 256, 3
Q, B = 16, 64
def parts(rng):
    X = rng.integers(0, 160, (N, 8, 16, V)) + 96 * rng.integers(0, 2, (N, 8, 1, V))
    p = rng.integers(0, 160, (N, 8, 16, S)) + 96 * rng.integers(0, 2, (N, 8, 1, S))
    return X, rng.integers(0, V, (N, 8, 16, C)), rng.integers(0, V, (N, 8, 16, S)), p, rng.integers(0, C, (N, 8, S))
def pack(X, K, M, p, c):
    return {"tx": np.ascontiguousarray(X.reshape(N, 128, V)).astype(BF), "kt": np.ascontiguousarray(K.reshape(N, 128, C)).astype(np.int32),
            "ms": np.ascontiguousarray(M.reshape(N, 128, S)).astype(np.int32), "z": np.ascontiguousarray(p.reshape(N, 128, S)).astype(BF), "cp": np.stack([gtable(a) for a in c])}
def setup_inputs(rng):
    return pack(*parts(rng))
def setup_inputs_spread(rng):
    X, K, M, p, c = parts(rng)
    X = np.minimum((np.exp2(8 * rng.random((N, 8, 1, V))) * rng.random((N, 8, 16, V))).astype(np.int64), 255)
    p = np.minimum((np.exp2(8 * rng.random((N, 8, 1, S))) * rng.random((N, 8, 16, S))).astype(np.int64), 255)
    K = np.minimum((V * rng.random((N, 8, 16, C)) ** 3).astype(np.int64), V - 1)
    M = np.minimum((V * rng.random((N, 8, 16, S)) ** 2).astype(np.int64), V - 1)
    c = np.minimum((C * rng.random((N, 8, S)) ** 2).astype(np.int64), C - 1)
    return pack(X, K, M, p, c)
def setup_inputs_ends(rng):
    half = (np.arange(16) >> 3)[:, None]
    X = 255 * rng.integers(0, 2, (N, 8, 16, V)); lo = 255 * rng.integers(0, 2, (N, 8, 1)); lo[:, 0] = 0; lo[:, 7] = 0
    for g in (0, 2, 4, 7):
        X[:, g, :, 0] = lo[:, g]; X[:, g, :, V - 1] = 255 - lo[:, g]
    p = 255 * rng.integers(0, 2, (N, 8, 16, S)); r = rng.integers(0, 4, (N, 8, 1, S)); p = np.where(r == 0, 0, np.where(r == 1, 255, p))
    K = rng.integers(0, 2, (N, 8, 16, C)); r = rng.integers(0, 5, (N, 8, 1, C))
    K = (V - 1) * np.where(r == 0, half, np.where(r == 1, 1 - half, np.where(r == 2, K[:, :, :1], K)))
    M = rng.integers(0, 2, (N, 8, 16, S)); r = rng.integers(0, 5, (N, 8, 1, S))
    M = (V - 1) * np.where(r == 0, half, np.where(r == 1, 1 - half, np.where(r == 2, M[:, :, :1], M)))
    c = np.where(rng.random((N, 8, S)) < 0.75, (C - 1) * rng.integers(0, 2, (N, 8, S)), rng.integers(0, C, (N, 8, S)))
    K[:, 7, :, C - 1] = V - 1; K[:, 0, :8, C - 1] = V - 1; K[:, 0, 8:, C - 1] = 0
    for g in (0, 7):
        for i in (0, 1, S - 1):
            p[:, g, :, i] = 0; c[:, g, i] = C - 1; M[:, g, :, i] = 0
        for i in (3, S - 5):
            p[:, g, :, i] = 0; c[:, g, i] = C - 1; M[:, g, :8, i] = 0; M[:, g, 8:, i] = V - 1
        for i in (2, S - 2):
            p[:, g, :, i] = 0; c[:, g, i] = C - 1; M[:, g, :, i] = V - 1
        for i in (4, S - 3):
            p[:, g, :, i] = 255; c[:, g, i] = C - 1; M[:, g, :, i] = 0
        for i in (5, S - 4):
            p[:, g, :, i] = 255; c[:, g, i] = C - 1; M[:, g, :8, i] = V - 1; M[:, g, 8:, i] = 0
    return pack(X, K, M, p, c)
def setup_inputs_corners(rng):
    X, K, M, p, c = parts(rng)
    c = rng.choice(np.array([0, 1, C // 2 - 1, C // 2, C - 2, C - 1]), (N, 8, S)); c[:, ::2] = (C - 1) * rng.integers(0, 2, (N, 4, S))
    X[:, 2] = rng.integers(0, 4, (N, 16, V)); p[:, 2] = rng.integers(0, 4, (N, 16, S))
    X[:, 5] = 8 * rng.integers(0, 32, (N, 16, V)); p[:, 5] = 8 * rng.integers(0, 32, (N, 16, S)); c[:, 5] = rng.integers(0, C, (N, S))
    K[:, 0] = rng.choice(np.array([0, 1, V - 1]), (N, 16, C)); M[:, 0, :, ::2] = 0; M[:, 0, :, 1::2] = V - 1
    M[:, 1] = Q * np.arange(S) + np.arange(16)[:, None] % Q
    M[:, 3] = np.take_along_axis(K[:, 3], c[:, 3][:, None, :], 2)
    K[:, 4] = K[:, 4, :1].copy(); M[:, 4, :, ::2] = M[:, 4, :1, ::2].copy()
    K[:, 6, 8:] = K[:, 6, :8].copy()
    kc = np.take_along_axis(K[:, 6, :1], c[:, 6][:, None, :], 2); near = np.take_along_axis(X[:, 6], kc, 2); p[:, 6, :, ::3] = near[:, :, ::3]
    p[:, 7] = np.take_along_axis(X[:, 7], M[:, 7, :1], 2)
    return pack(X, K, M, p, c)
def setup_inputs_crowd(rng):
    X, K, M, p, c = parts(rng); far1 = Q * B + 1
    for q in range(N):
        for g in range(7):
            o = rng.permutation(V)
            if g == 4:
                j = int(np.flatnonzero(o == far1)[0]); o[j] = o[B]; o[B] = far1
                X[q, g, :, far1] = 255 * (q & 1); X[q, g, 0, far1 + 1] = 0
                X[q, g, :, far1 + 2] = X[q, g, :, far1 + 1]; X[q, g, 0, far1 + 2] = S - 1
            own, far = o[:S], o[S:]
            M[q, g] = own[None, :]; p[q, g] = np.minimum(X[q, g][:, own] + rng.integers(0, 8, (16, S)), 255)
            two = rng.permutation(C)[:2]
            if g == 3: two = np.array([C - 1, C - 1])
            if g == 4:
                two = 1 + rng.permutation(C - 1)[:2]
                p[q, g, :, B] = X[q, g, :, far1]; K[q, g, :8, 0] = far1 + 1; K[q, g, 8:, 0] = far1 + 2
            if g in (2, 6):
                c[q, g] = two[rng.integers(0, 2, S)]; K[q, g, :, two[0]] = far[:16]; K[q, g, :, two[1]] = far[16:32]
            else:
                c[q, g] = two[0]; K[q, g, :, two[0]] = np.concatenate([far[:8], far[:8]])
            if g in (1, 5):
                i = 0 if g == 1 else S - 1
                M[q, g, :, i] = K[q, g, :, two[0]]
        full, near, home = [int(v) for v in rng.permutation(V)[:3]]
        X[q, 7, :, full] = 255; X[q, 7, :, near] = 255; X[q, 7, int(rng.integers(0, 16)), near] = 254; X[q, 7, :, home] = rng.integers(0, 8, 16)
        c[q, 7] = rng.integers(1, C // 2 - 1, S) + (C // 2) * rng.integers(0, 2, S)
        for i in (0, S - 2, S - 1): p[q, 7, :, i] = 0
        c[q, 7, 0] = 0; M[q, 7, :, 0] = home; K[q, 7, :8, 0] = full; K[q, 7, 8:, 0] = near
        c[q, 7, S - 1] = C - 1; M[q, 7, :, S - 1] = home; K[q, 7, :8, C - 1] = near; K[q, 7, 8:, C - 1] = full
        c[q, 7, S - 2] = C // 2; M[q, 7, :, S - 2] = near; M[q, 7, 0, S - 2] = full; K[q, 7, :, C // 2] = home
    return pack(X, K, M, p, c)
def check_inputs(d):
    bad = []
    for k, hi in (("tx", 255), ("kt", V - 1), ("ms", V - 1), ("z", 255), ("cp", C - 1)):
        v = np.asarray(d[k]).astype(np.float64)
        if not (np.min(v) >= 0 and np.max(v) <= hi): bad.append("range of " + k)
        elif np.any(v != np.floor(v)): bad.append("whole numbers of " + k)
    return bad
def mixed(p):
    return np.add.reduce(p * (2 * np.arange(16) + 1)[:, None], axis=-2)
def travel(v):
    w = v.reshape(v.shape[:-1] + (N, B)); o = np.empty_like(w)
    for h in range(N): o[..., (h + 1) % N, :] = np.roll(w[..., h, :], h, axis=0)
    return o.reshape(v.shape)
def reference(tx, kt, ms, z, cp):
    X = tx.astype(np.float32).astype(np.int64).reshape(N, 8, 16, V); K = kt.astype(np.int64).reshape(N, 8, 16, C); M = ms.astype(np.int64).reshape(N, 8, 16, S)
    p = z.astype(np.float32).astype(np.int64).reshape(N, 8, 16, S); c = np.stack([gentries(a) for a in cp]).astype(np.int64)
    A = np.zeros((N, 8), np.int64); row = np.arange(16)[:, None]; slot = np.arange(S)
    for rnd in range(RO):
        kc = np.take_along_axis(K, c[:, :, None, :], 3)
        x = np.take_along_axis(X, kc.reshape(N, 8, 1, 16 * S), 3).reshape(N, 8, 16, 16, S)
        m = np.take_along_axis(X, M.reshape(N, 8, 1, 16 * S), 3).reshape(N, 8, 16, 16, S)
        d = np.add.reduce(np.abs(x - p[:, :, :, None, :]), axis=2); dm = np.add.reduce(np.abs(m - p[:, :, :, None, :]), axis=2)
        s0, s1 = np.add.reduce(d[:, :, :8], axis=2), np.add.reduce(d[:, :, 8:], axis=2)
        t0, t1 = np.add.reduce(dm[:, :, :8], axis=2), np.add.reduce(dm[:, :, 8:], axis=2)
        b = (s1 < s0).astype(np.int64); e = np.argmin(dm, axis=2); a = np.argmax(d, axis=2)
        db = np.where(b[:, :, None, :] == 1, d[:, :, 8:], d[:, :, :8]); w = 8 * b + np.argmin(db, axis=2)
        trust = np.abs(s1 - s0) >= np.abs(t1 - t0) + 8 * A[:, :, None]
        contra = trust & (np.min(dm, axis=2) < np.min(db, axis=2)); agree = trust & ~contra
        me = np.take_along_axis(m, e[:, :, None, None, :], 3)[:, :, :, 0]; xw = np.take_along_axis(x, w[:, :, None, None, :], 3)[:, :, :, 0]
        name = np.take_along_axis(M, e[:, :, None, :], 2)[:, :, 0]; u = mixed(p)
        take = agree[:, :, None, :] & ((row >> 3) == b[:, :, None, :]) & (d < dm)
        fresh = ~trust[:, :, None, :] & (16 * dm > (t0 + t1)[:, :, None, :])
        M = np.where(take, kc, np.where(fresh, (kc + u[:, :, None, :] + 37 * row) & (V - 1), M))
        t = (2 * c + 1 - b) & (C - 1)
        for q in range(N):
            for g in range(8):
                i = np.flatnonzero(contra[q, g]); col, first = np.unique(t[q, g, i], return_index=True); i = i[first]
                K[q, g, a[q, g, i], col] = name[q, g, i]
        p = np.where(agree[:, :, None, :], (p + xw) >> 1, np.abs(p - me)); u = mixed(p)
        own = np.repeat((Q * slot + (u & (Q - 1)))[:, :, None, :], 16, axis=2)
        np.put_along_axis(X, own, (np.take_along_axis(X, own, 3) + p) >> 1, 3)
        if rnd < RO - 1:
            A = np.add.reduce(contra.astype(np.int64), axis=2)
            c = np.where(agree, (2 * c + b) & (C - 1), u & (C - 1))
            p = travel(p); M = travel(M); c = travel(c)
    return {"ytx": X.reshape(N, 128, V).astype(BF), "ykt": K.reshape(N, 128, C).astype(np.float32), "yms": M.reshape(N, 128, S).astype(np.float32), "yz": p.reshape(N, 128, S).astype(BF)}

@@ -1,0 +1,509 @@
+from concourse.bass import DstId, RemoteDMATransfer
+from concourse.mybir import AluOpType as ALU, ActivationFunctionType as AF
+
+RO, NB, ROW = 3, 4, 136
+ZERO = 4096
+ZB, ZH = 4096, 4352
+N4 = [3, 4, 4]
+KORD = [2, 3, 0, 1, 4, 5, 6, 7]
+FS = [16, 16, 0]
+SAME = True
+BIG = 1.0e6
+ORDER = "0004050602030<010@1H0A0H080F0L0M0I190E0G0N0K090J180C0B0D071>151L0=140;100>0W0:0O1M121R0P0?1W1U1=0R231@0S1J270T241K210U1?1Q0V113P16291:1P1;1S1B1C1V1A3?1O130Q25221I171T1N281<201D261E1F3O1G3R3W3V2<2=2;2@2G2W2J2H2B2A2K302D2>37382C2E2M2?3<3;2Q2N332L2O342I312S2F322R2U352P3N392V3M2:2T36413=4243443A3Q3S3U3:5746453@3>474;4:5849483C4<3B4=594>4A4?4@4B3D3T4D404F4P4E4C4G3G3E4H5:4I5;3F5V4J625L60635>4K5O5B5M4L5Q3J5?4M5P5<3H615U5G3K5T5E5A4O3I5D6@5=5K4R5J515@4S5N523L5I5R5C535S4N5W5F5H6L6K4T6P6I4Q6F6M6U546T6G6S6O6H6R4U6N556Q4V6J68645665666A696C506B6:7R4W677S6;6D6E7B6<7I6=747<8F6V7:7H706>797273767A758G6?7771787=7;7D7F8W7@7>7N7M7E827K927?7J7L7C7G9?8085836W84867T87818H8I7O7U7V8R888K7P8S7W9>8D898B8;8N8O8@8E8<8C8>8J8:8U8=9A7Q9=8?8T9F9@9E9B9<8A8L9C9D9G:N8P9H:O8Q9I9L9J9K909M8V8M9N:P939R919O9Q9P9S9T9U9V96:0949W:1:2:3;L95:597:?:498:6:7:Q:R;K99:8;M9:;A;0:9;=;6;4;I;5;F::;;9;;H;C;@:;;8:=;D:<:S;E;3:T;N:V;>;7:>;1:@;9;W;G;<:A:H;J:B;::I:U:C;?:J;B:D:K:W:E;2<7<C<><;;O<D:G<B:L<?<@;P<A:M<=<6<9<8<:<5<<<0<2<1;Q=A:FAC;R<3=B;S=0=:;T=<<W<E;U<G>5<I<S<P<V<H=1<J=3<K;V<O<L>6<M<T=8<N=4<Q=6<F==<R=2=;=I=5=9<U=7<4=E=L=J=K=M=C=F=N=>=D>7=G>==O>9=?=H=P>U>3=U=R>A>1>4=S=V>>=W>2=Q>C>V>S>T=T?0>W?5?3>0?4?2>;?1?6=@?7?8>??9?:>E>F>B?;@4?<>:?=@5?A?@???>?B>G?C?D?E?F>J?G?H?I?JA2?L?K>I?M?N@7?O@8>8>K?P@9@N>D@O@G?Q@K@:A1?R>N?SA>@L>O@W@?@M>@@;?U@S?V@E@H?W@VA0@0><@T@1@J@F@B@A@Q>H@2@3@<>L@U@@@>@C@P@R@I@=@D@6A?A5>PA3A6A7A8>MA4A9A:A;A<>Q>R?TA@A=AAAB"
+
+
+def _sb(n, d):
+    return ("sbuf", [128] + (n if isinstance(n, list) else [n]), d)
+
+
+F, H, I, U, Q = "float32", "bfloat16", "int32", "uint16", "float16"
+SCRATCH = {
+    "X": _sb(4096, H), "W": _sb(4112, H), "Dm": _sb(4608, H), "zrep": _sb(4096, H),
+    "adM": _sb([16, 256], H), "adK": _sb([16, 256], H),
+    "kti": _sb(1024, I), "K": _sb(1280, F), "msi": _sb(256, I), "cpi": _sb(16, I),
+    "L0": _sb([NB, ROW], U), "L1": _sb([NB, ROW], U), "L2": _sb([NB, ROW], U),
+    "S0": _sb([NB, ROW], U), "S1": _sb([NB, ROW], U),
+    "QW": _sb(768, I), "kcu": _sb(256, U), "kc4": _sb(256, F), "km": _sb(256, F), "kk": _sb(256, F),
+    "P2s": _sb(256, F), "q1": _sb(256, F), "nMi": _sb(256, I), "nMf": _sb(256, F),
+    "G2": _sb(256, H), "v2": _sb(256, Q), "zn": _sb(256, H), "sx": _sb(256, Q), "sxu": _sb(256, U),
+    "krep": _sb(256, F), "eE": _sb(256, F), "Xn": _sb(256, F), "eA": _sb(256, F), "old": _sb(256, F), "Y": _sb(256, F),
+    "junk": _sb(2048, H), "s12": _sb(32, F), "nb": _sb(16, F),
+    "scm": _sb(256, I), "sct": _sb(256, F), "sck": _sb(512, I), "scs": _sb(256, F),
+    "cu": _sb(16, U), "c2": _sb(32, I), "TT": _sb(32, I), "tD": _sb(32, F),
+    "ei": _sb(16, I), "eu": _sb(16, U), "mt": _sb(16, F), "dE": _sb(16, F),
+    "aDT": _sb(16, F), "thP": _sb(16, F), "tm": _sb(16, F), "thN": _sb(16, F), "Ac": _sb(4, F), "aj": _sb(16, F),
+    "UU": _sb(32, F), "GG": _sb(32, F), "wa": _sb(64, I), "pK": _sb(32, F),
+    "P": _sb(160, F), "R": _sb(112, F), "BASE": _sb(64, F), "LF": _sb(64, F), "LU": _sb(64, U),
+    "au": _sb(16, U), "nag": _sb(16, F),
+    "ui": _sb(16, I), "u15": _sb(16, I), "vf": _sb(16, F), "vu": _sb(16, U),
+    "c1": _sb(16, F), "ci": _sb(16, I), "cn": _sb(16, I),
+    "eq": _sb(16, F), "of1": _sb(16, F), "of2": _sb(16, F), "ofu": _sb(16, U),
+    "ones": _sb(256, F), "pi": _sb(1, I), "fi": _sb(1, I), "col": _sb(8, F), "If": _sb(128, F), "Bt": _sb(128, F),
+    "Bf": _sb(128, F), "srow": _sb(128, F), "Ht": _sb(128, F), "Hm": _sb(128, F), "P2m": _sb(128, F), "t2": _sb(128, F),
+    "Ip": _sb(128, F), "In": _sb(128, F), "Inf": _sb(128, F),
+    "Ib": _sb(128, H), "Inb": _sb(128, H), "I37": _sb(128, H), "Ub": _sb(128, H),
+    "Z": _sb(144, H), "ZU": _sb(144, H), "ktab": _sb(128, H), "kcol": _sb(256, H),
+    "r16": _sb(256, F), "r8": _sb(256, F), "rx": _sb(256, F), "rs": _sb(256, F),
+    "Et": _sb(32, F), "E": _sb(32, F), "tab": _sb(1280, F), "iF": _sb(256, F), "i0": _sb(16, F), "iL": _sb(16, F),
+    "c16": _sb(16, F), "pKc": _sb(32, F), "zp": _sb(48, F), "i256": _sb(16, F),
+    "ps": ("psum", [128, 4096], F),
+}
+SEMAPHORES = ["v", "a", "p", "g", "ldx", "ldk", "ldm", "ldz", "ldc", "arr0", "arr1", "snt0", "snt1",
+              "ox", "ok", "om", "oz"]
+
+
+def engine_split(topo, src, dsts):
+    off = [d for d in dsts if topo.chip(d) != topo.chip(src)]
+    on = [d for d in dsts if topo.chip(d) == topo.chip(src)]
+    used, res = [], {}
+    for part in (off, on):
+        if not part:
+            continue
+        free = [e for e in topo.engines(src, part[0]) if e not in used]
+        n = 1
+        while 2 * n * len(part) <= len(free):
+            n *= 2
+        for j, d in enumerate(part):
+            res[d] = free[j * n:(j + 1) * n]
+            used = used + res[d]
+    return res
+
+
+def ordered(ops):
+    if len(ORDER) != 2 * len(ops):
+        return ops
+    return [ops[(ord(ORDER[j]) - 48) * 40 + ord(ORDER[j + 1]) - 48] for j in range(0, len(ORDER), 2)]
+
+
+def emit(g, T, ops):
+    q = {"v": g.vector, "a": g.scalar, "p": g.tensor, "g": g, "s": g.sync}
+    last_w, readers, bank = {}, {}, {}
+    clock = {e: {} for e in q}
+    done, waits, marked = [], [], set()
+    for n, o in enumerate(ops):
+        e = o["e"]
+        if o["f"] is None and o["sem"]:
+            waits.append([])
+            done.append({o["sem"][0]: n})
+            for k in o["w"]:
+                last_w[k] = n
+                readers[k] = []
+            continue
+        deps, over = set(), set()
+        for k in o["r"]:
+            if k in last_w:
+                deps.add(last_w[k])
+        for k in o["w"]:
+            if k in last_w:
+                over.add(last_w[k])
+            over.update(readers.get(k, []))
+        deps.update(m for m in over if SAME or ops[m]["e"] != e or ops[m]["sem"] or o["sem"])
+        for b in o["b"]:
+            deps.update(m for f, m in bank.get(b, {}).items() if f != e)
+        ws = []
+        for m in sorted(deps, reverse=True):
+            p = ops[m]
+            if p["e"] == "p" and e == "p":
+                continue
+            key = p["sem"][0] if p["sem"] else p["e"]
+            if clock[e].get(key, -1) >= m:
+                continue
+            ws.append(m)
+            marked.add(m)
+            for k2, v2 in done[m].items():
+                if clock[e].get(k2, -1) < v2:
+                    clock[e][k2] = v2
+        waits.append(ws)
+        d = dict(clock[e])
+        d[o["sem"][0] if o["sem"] else e] = n
+        done.append(d)
+        for k in o["r"]:
+            readers.setdefault(k, []).append(n)
+        for k in o["w"]:
+            last_w[k] = n
+            readers[k] = []
+        for b in o["b"]:
+            bank.setdefault(b, {})[e] = n
+    cnt, val = {e: 0 for e in q}, {}
+    for n, o in enumerate(ops):
+        e = o["e"]
+        for m in waits[n]:
+            p = ops[m]
+            if p["sem"]:
+                q[e].wait_ge(T.sem[p["sem"][0]], p["sem"][1])
+            else:
+                q[e].wait_ge(T.sem[p["e"]], val[m])
+        if o["f"] is None:
+            continue
+        ins = o["f"]()
+        if o["sem"]:
+            if ins is not None:
+                ins.then_inc(T.sem[o["sem"][0]], o["sem"][1])
+        elif n in marked:
+            cnt[e] += 1
+            val[n] = cnt[e]
+            ins.then_inc(T.sem[e], 1)
+
+
+def rank_program(g, core, T, topo):
+    rank = T.rank_of(core)
+    if rank is None:
+        return
+    cores = list(T.cores)
+    n = len(cores)
+    V, A, PE = g.vector, g.scalar, g.tensor
+    ops = []
+
+    def op(e, f, r, w, b=(), sem=None):
+        ops.append({"e": e, "f": f, "r": list(r), "w": list(w), "b": list(b), "sem": sem})
+
+    def cp(out, in_, r, w, b=()):
+        op("v", lambda: V.tensor_copy(out, in_), r, w, b)
+
+    def tt(out, a, c, o, r, w, b=()):
+        op("v", lambda: V.tensor_tensor(out, a, c, o), r, w, b)
+
+    def ts(out, a, s1, s2, o0, o1, r, w, b=()):
+        if s2 is None:
+            op("v", lambda: V.tensor_scalar(out, a, s1, None, o0), r, w, b)
+        else:
+            op("v", lambda: V.tensor_scalar(out, a, s1, s2, o0, o1), r, w, b)
+
+    def ms(out, c, w):
+        op("v", lambda: V.memset(out, c), [], w)
+
+    def scan(out, d0, d1, o0, o1, r, w, b):
+        op("v", lambda: V.tensor_tensor_scan(out, d0, d1, 0.0, o0, o1), r, w, b)
+
+    def act(out, in_, fn, r, w, b=(), bias=0.0, scale=1.0, acc=None):
+        op("a", lambda: A.activation(out, in_, fn, bias=bias, scale=scale, accum_out=acc), r, w, b)
+
+    def aff(out, in_, scale, bias, r, w, b=()):
+        act(out, in_, AF.Identity, r, w, b, bias=bias, scale=scale)
+
+    group = []
+
+    def mm(out, l, rh, st, sp, r, w, b):
+        group.append((out, l, rh, st, sp, r))
+        if sp:
+            part = list(group)
+            del group[:]
+
+            def run():
+                for m in part:
+                    ins = PE.matmul(*m[:5])
+                return ins
+            op("p", run, [k for m in part for k in m[5]], w, b)
+
+    def iota(out, pat, base, cm, w, small=True):
+        if small:
+            op("g", lambda: g.iota(out, pat, base, cm, allow_small_or_imprecise_dtypes=True), [], w)
+        else:
+            op("g", lambda: g.iota(out, pat, base, cm), [], w)
+
+    def asel(out, in_, pat, o, fill, base, cm, r, w):
+        op("g", lambda: g.affine_select(out, in_, pat, o, fill, base, cm), r, w)
+
+    def dma(e, out, in_, r, w, sem):
+        qq = g.sync if e == "s" else g.scalar
+        op(e, lambda: qq.dma_start(out, in_), r, w, sem=(sem, 16))
+
+    def bk(b, a=0, c=256):
+        return T.ps[:, 512 * b + a:512 * b + c]
+
+    W, X, K, Dm = T.W, T.X, T.K, T.Dm
+    zb = Dm[:, ZB:ZB + 256]
+    add, sub, mul, mx, mn = ALU.add, ALU.subtract, ALU.mult, ALU.max, ALU.min
+    band = ALU.bitwise_and
+    ones, col = T.ones, T.col
+
+    dma("a", zb, T.z[:], [], ["zb"], "ldz")
+    dma("a", T.msi[:], T.ms[:], [], ["msi"], "ldm")
+    dma("a", T.cpi[:], T.cp[:], [], ["cpi"], "ldc")
+    dma("s", X[:], T.tx[:], [], ["X"], "ldx")
+    dma("s", T.kti[:], T.kt[:], [], ["kti"], "ldk")
+    loads = len(ops)
+
+    ms(ones[:], 1.0, ["ones"])
+    iota(T.pi[:], [[0, 1]], 0, 1, ["pi"], False)
+    asel(T.If[:], ones[:, 0:128], [[-1, 128]], ALU.is_equal, 0.0, 0, 1, ["ones"], ["If"])
+    asel(T.Bt[:], ones[:, 0:128], [[16, 8], [0, 16]], ALU.is_ge, 0.0, 15, -1, ["ones"], ["Bt"])
+    asel(T.Bf[:], T.Bt[:], [[-16, 8], [0, 16]], ALU.is_ge, 0.0, 0, 1, ["Bt"], ["Bf"])
+    iota(T.ktab[:], [[16, 2], [0, 4], [1, 16]], 0, 0, ["ktab"])
+    iota(T.i0[:], [[16, 16]], 0, 0, ["i0"])
+    iota(T.srow[:], [[0, 8], [-2, 2], [0, 8]], 1, 0, ["srow"])
+    iota(T.Et[:, 0:16], [[1, 16]], 0, 0, ["Et0"])
+    iota(T.Et[:, 16:31], [[-1, 15]], 14, 0, ["Et1"])
+    iota(T.tab[:], [[1, 1280]], 0, 0, ["tab"])
+    ms(T.Z[:], 0.0, ["Z"])
+    ms(T.ZU[:], 0.0, ["ZU"])
+    ms(W[:, ZERO:ZERO + 16], 0.0, ["W0"])
+    ms(T.S0[:, :, 132:136], 0, ["S0p"])
+    ms(T.S1[:, :, 132:136], 0, ["S1p"])
+    ms(T.Et[:, 31:32], 15.0, ["Et2"])
+    ms(T.Ac[:, 1:2], 64.0, ["A64"])
+    ms(T.Ac[:, 2:3], -1.0, ["Am1"])
+    ts(T.fi[:], T.pi[:], 15, None, band, None, ["pi"], ["fi"])
+    ms(T.BASE[:, 32:48], float(ZERO), ["B2"])
+    cp(col[:, 0:1], T.fi[:], ["fi"], ["c0"])
+    ts(col[:, 1:2], T.fi[:], 2.0, 1.0, mul, add, ["fi"], ["c1_"])
+    ts(col[:, 2:3], T.fi[:], 7.5, 2.0, ALU.is_gt, mul, ["fi"], ["c2_"])
+    for buf, c in ((T.r16, 0.0), (T.r8, 0.0), (T.rx, 2.0), (T.rs, 1.0)):
+        aff(buf[:], ones[:], c, 0.0, ["ones"], ["rr"])
+    aff(K[:, 1024:1280], ones[:], 0.0, 0.0, ["ones"], ["Kd"])
+    for o_, k_, c in ((T.r16[:, 0::16], 16, BIG), (T.r8[:, 0::8], 32, BIG), (T.rx[:, 0::16], 16, -BIG),
+                      (T.rs[:, 0::16], 16, 0.0), (T.rs[:, 8::16], 16, -1.0)):
+        aff(o_, ones[:, 0:k_], c, 0.0, ["ones", "rr"], ["rr"])
+    aff(T.Ib[:], T.If[:], 1.0, 0.0, ["If"], ["Ib"])
+    aff(T.Inb[:], T.If[:], -1.0, 0.0, ["If"], ["Inb"])
+    aff(T.I37[:], T.If[:], 37.0, 0.0, ["If"], ["I37"])
+    aff(T.Z[:, 15:128:16], T.Bf[:, 0::16], 16.0, 0.0, ["Bf", "Z"], ["Z"])
+    aff(T.ZU[:, 15:128:16], T.Bf[:, 0::16], col[:, 1:2], 0.0, ["Bf", "ZU", "c1_"], ["ZU"])
+    aff(T.Ub[:], T.Bf[:], col[:, 1:2], 0.0, ["Bf", "c1_"], ["Ub"])
+    aff(T.kcol[:], ones[:], col[:, 0:1], 0.0, ["ones", "c0"], ["kcol"])
+    aff(T.t2[:], T.Bf[:], -2.0 ** 17, 0.0, ["Bf"], ["t2"])
+    asel(T.P2m[:], T.t2[:], [[-1, 128]], ALU.not_equal, 15 * 2.0 ** 17, 0, 1, ["t2"], ["P2m"])
+    ts(col[:, 3:4], col[:, 2:3], -1.0, 1.0 / 32, add, mul, ["c2_"], ["c3_"])
+    ts(col[:, 4:5], col[:, 2:3], -1.0, 16384.0, add, mul, ["c2_"], ["c4_"])
+    aff(T.Ip[:], T.If[:], 16384.0, 0.0, ["If"], ["Ip"])
+    aff(T.In[:], T.If[:], -16384.0, 0.0, ["If"], ["In"])
+    aff(T.Inf[:], T.If[:], -1.0, 0.0, ["If"], ["Inf"])
+    aff(T.iL[:], T.i0[:], 1.0, col[:, 0:1], ["i0", "c0"], ["iL"])
+    aff(T.Ht[:], T.Bf[:], col[:, 4:5], 0.0, ["Bf", "c4_"], ["Ht"])
+    aff(T.c16[:], T.iL[:], 16.0, 0.0, ["iL"], ["c16"])
+    aff(T.BASE[:, 48:64], T.iL[:], 1.0, 1024.0, ["iL"], ["B3"])
+    aff(T.BASE[:, 16:32], T.iL[:], 3.0, 1.0, ["iL"], ["B1"])
+    for r in range(RO):
+        a4 = 2 * N4[r]
+        aff(T.zp[:, 16 * r:16 * r + a4], T.iL[:, 0:a4], 1.0, float(ZH), ["iL"], ["zpa%d" % r])
+        aff(T.zp[:, 16 * r + a4:16 * r + 16], T.iL[:, a4:16], 1.0, float(ZB), ["iL"], ["zpb%d" % r])
+    aff(Dm[:, ZH:ZH + 256], ones[:], 0.0, 0.0, ["ones"], ["zh"])
+    aff(T.i256[:], T.iL[:], 1.0 / 256, 0.0, ["iL"], ["i256"])
+    for h in range(2):
+        aff(T.pKc[:, h::2], T.iL[:], 16.0, -float(ZERO), ["iL"], ["pKc%d" % h])
+    tt(T.Hm[:], T.Ht[:], T.srow[:], mul, ["Ht", "srow"], ["Hm"])
+    ts(T.E[:], T.Et[:], col[:, 0:1], None, ALU.is_equal, None, ["Et0", "Et1", "Et2", "c0"], ["E"])
+    aff(T.iF[:], T.tab[:, 0:256], 1.0 / 256, 1.0 / 512, ["tab"], ["iF"])
+
+    dsts = [cores[(rank + h) % n] for h in range(1, n)]
+    eng = engine_split(topo, core, dsts)
+    arrivals = 0
+    for h in range(1, n):
+        s = (rank - h) % n
+        arrivals += len(engine_split(topo, cores[s], [cores[(s + j) % n] for j in range(1, n)])[core])
+
+    def spread(src, r, h, m, on):
+        for k in range(16):
+            o = T.zrep[:, 1024 * h + k:1024 * (h + m):16]
+            keys = ["zr%d_%d" % (j, k) for j in range(h, h + m)]
+            if k < on:
+                aff(o, src, 1.0, 0.0, r, keys)
+            else:
+                cp(o, src, r, keys)
+
+    def zr(u, m=1):
+        return T.zrep[:, 512 * u:512 * (u + m)]
+
+    def zk(h):
+        return ["zr%d_%d" % (h, k) for k in range(16)]
+
+    Mi = T.QW[:, 2::3]
+    P, R = T.P, T.R
+
+    for r in range(RO):
+        last = r == RO - 1
+        Lr = T["L%d" % r]
+        n4 = N4[r]
+        if r == 0:
+            spread(zb, ["zb"], 0, NB, 0)
+            cp(T.cu[:], T.cpi[:], ["cpi"], ["cu"])
+            cp(Lr[:, :, 0:64], T.msi[:], ["msi"], ["Lm"])
+            cp(Mi, T.msi[:], ["msi"], ["Mi"])
+            cp(K[:, 0:1024], T.kti[:], ["kti"], ["K"])
+            cp(T.kcu[:], T.kti[:].indirect(T.cu[:]), ["kti", "cu"], ["kcu%d" % h for h in range(NB)])
+        else:
+            cp(T.kcu[:, 64:128], K[:, 0:1024].indirect(Lr[:, 1, 128:132]), ["K", "Lown"], ["kcu1"])
+            cp(T.kcu[:, 0:64], K[:, 0:1024].indirect(Lr[:, 0, 128:132]), ["K", "arr"], ["kcu0"])
+            cp(T.kcu[:, 128:256], K[:, 0:1024].indirect(T.cu[:, 8:16]), ["K", "cu"], ["kcu2", "kcu3"])
+            cp(Mi, Lr[:, :, 0:64], ["arr", "Lown"], ["Mi"])
+
+        for h in (1, 0, 2, 3):
+            us = [2 * h, 2 * h + 1]
+            d = Dm[:, 1024 * h:1024 * h + 1024]
+            tt(d, X[:].indirect(Lr[:, h, 0:64]), zr(2 * h, 2), sub,
+               ["X", "Lm" if r == 0 else "Lown" if h == 1 else "arr"] + zk(h), ["Dm%d" % h])
+            act(T.adM[:, 4 * h:4 * h + 4, :], d, AF.Abs, ["Dm%d" % h], ["aM%d" % u for u in us])
+        for j in range(8):
+            u = KORD[j] if r else j
+            d = W[:, 512 * u:512 * u + 512]
+            o = T.adK[:, 2 * u:2 * u + 2, :]
+            x = X[:].indirect(T.kcu[:, 32 * u:32 * u + 32])
+            if u < n4:
+                b, bw = ((4, ["p44", "uL"]), (5, ["p45"]), (7, ["P1", "Hs"]))[j % 3]
+                aff(d, x, 1.0, 0.0, ["X", "kcu%d" % (u // 2)], ["Wk%d" % u])
+                mm(bk(b, 0, 512), T.Ib[:], d, True, False, ["Ib", "Wk%d" % u], bw, [b])
+                mm(bk(b, 0, 512), T.Inb[:], zr(u), False, True, ["Inb"] + zk(u // 2), bw, [b])
+                act(o, bk(b, 0, 512), AF.Abs, bw, ["aK%d" % u], [b])
+            else:
+                tt(d, x, zr(u), sub, ["X", "kcu%d" % (u // 2)] + zk(u // 2), ["Wk%d" % u])
+                act(o, d, AF.Abs, ["Wk%d" % u], ["aK%d" % u])
+        for h in (1, 0, 2, 3):
+            for t in range(2):
+                ad = T.adM if t == 0 else T.adK
+                rd = ["Z", "a%s%d" % ("MK"[t], 2 * h), "a%s%d" % ("MK"[t], 2 * h + 1)]
+                o = bk(t, 64 * h, 64 * h + 64)
+                mm(o, T.Ib[:], T.ktab[:, 64 - 64 * t:128 - 64 * t], True, False, ["Ib", "ktab"], [], [t])
+                for b in range(16):
+                    mm(o, T.Z[:, 15 - b:143 - b], ad[:, 4 * h:4 * h + 4, 16 * b:16 * b + 16], False, b == 15,
+                       rd, ["key%d_%d" % (t, h)], [t])
+                o = bk(2 + t, 64 * h, 64 * h + 64)
+                for k in range(16):
+                    mm(o, T.Z[:, 15 - k:143 - k], ad[:, 4 * h:4 * h + 4, k::16], k == 0, k == 15,
+                       rd, ["d%d_%d" % (t, h)], [2 + t])
+        KM, KK, DM, DK = (["%s_%d" % (x, h) for h in range(NB)] for x in ("key0", "key1", "d0", "d1"))
+
+        aff(Dm[:, ZH:ZH + 32 * n4], Dm[:, ZB:ZB + 32 * n4], 0.5, 0.0, ["zb"], ["zh"])
+        act(T.kc4[:], K[:, 0:1024].indirect(T.cu[:]), AF.Identity, ["K", "cu"], ["kc4"], bias=4096.0)
+        aff(T.km[:], bk(2), 1.0 / 16, -1.0 / 16, DM, ["km"], [2])
+        aff(T.kk[:], bk(3), 1.0 / 16, col[:, 3:4], DK + ["c3_"], ["kk"], [3])
+        mm(bk(6), T.Ub[:], zb, True, False, ["Ub", "zb"], ["fr"], [6])
+        mm(bk(6), T.I37[:], T.kcol[:], False, False, ["I37", "kcol"], ["fr"], [6])
+        mm(bk(6), T.If[:], T.kc4[:], False, True, ["If", "kc4"], ["fr"], [6])
+        mm(bk(6, 256, 512), T.P2m[:], T.km[:], True, True, ["P2m", "km"], ["P2"], [6])
+        aff(T.P2s[:], bk(6, 256, 512), 1.0, 0.0, ["P2"], ["P2s"], [6])
+        mm(bk(7), T.Ip[:], T.km[:], True, False, ["Ip", "km"], ["P1"], [7])
+        mm(bk(7), T.In[:], T.kk[:], False, True, ["In", "kk"], ["P1"], [7])
+        mm(bk(7, 256, 512), T.Hm[:], T.kk[:], True, True, ["Hm", "kk"], ["Hs"], [7])
+        tt(bk(6), bk(6), T.P2s[:], mn, ["P2s", "fr"], ["fr"], [6])
+        tt(T.QW[:, 1::3], bk(6), Mi, mx, ["fr", "Mi"], ["QB"], [6])
+        tt(T.q1[:], bk(7), T.kc4[:], mn, ["P1", "kc4"], ["q1"], [7])
+        tt(bk(7, 256, 512), bk(7, 256, 512), T.q1[:], mn, ["Hs", "q1"], ["Hs"], [7])
+        tt(T.QW[:, 0::3], bk(7, 256, 512), Mi, mx, ["Hs", "Mi"], ["QA"], [7])
+
+        scan(T.sct[:], T.rs[:], bk(0), mul, add, ["rr"] + KM, ["sct"], [0])
+        scan(T.scm[:], T.r16[:], bk(0), add, mn, ["rr"] + KM, ["scm"], [0])
+        for h in range(2):
+            ts(T.c2[:, h::2], T.cu[:], 2.0, float(h), mul, add, ["cu"], ["c2%d" % h])
+        ts(T.ei[:], T.scm[:, 15::16], 15, None, band, None, ["scm"], ["ei"])
+        ts(T.TT[:], T.c2[:], 1023, None, band, None, ["c20", "c21"], ["TT"])
+        cp(T.eu[:], T.ei[:], ["ei"], ["eu"])
+        tt(T.BASE[:, 0:16], T.ei[:], T.c16[:], add, ["ei", "c16"], ["B0"])
+        tt(T.mt[:], T.scm[:, 15::16], T.ei[:], sub, ["scm", "ei"], ["mt"])
+        for h in range(2):
+            tt(T.tD[:, h::2], T.TT[:, 1 - h::2], T.BASE[:, 48:64], sub, ["TT", "B3"], ["tD%d" % h])
+        tt(T.dE[:], T.zp[:, 16 * r:16 * r + 16], T.BASE[:, 0:16], sub, ["zpa%d" % r, "zpb%d" % r, "B0"], ["dE"])
+        act(T.aDT[:], T.sct[:, 15::16], AF.Abs, ["sct"], ["aDT"], bias=-64.0)
+        act(T.tm[:], T.aDT[:], AF.Relu, ["aDT", "Am1"], ["tm"], bias=T.Ac[:, 2:3])
+        aff(T.thP[:], T.aDT[:], 1.0, T.Ac[:, 1:2], ["aDT", "A64"], ["thP"])
+        aff(T.thN[:], T.tm[:], -1.0, 63.0, ["tm"], ["thN"])
+        scan(T.scs[:], T.rs[:], bk(1), mul, add, ["rr"] + KK, ["scs"], [1])
+        scan(T.sck[:, 0:256], T.r8[:], bk(1), add, mn, ["rr"] + KK, ["sck"], [1])
+        scan(T.sck[:, 256:512], T.rx[:], bk(1), add, mx, ["rr"] + KK, ["scx"], [1])
+        tt(T.UU[:, 0::2], T.scs[:, 15::16], T.thP[:], ALU.is_ge, ["scs", "thP"], ["U0"])
+        tt(T.UU[:, 1::2], T.scs[:, 15::16], T.thN[:], ALU.is_le, ["scs", "thN"], ["U1"])
+        for h in range(2):
+            tt(T.GG[:, h::2], T.sck[:, 7 + 8 * h:256:16], T.mt[:], ALU.is_lt, ["sck", "mt"], ["GG%d" % h])
+        ts(T.wa[:], T.sck[:, 7::8], 15, None, band, None, ["sck", "scx"], ["wa"])
+        AG, CH = P[:, 96:128], P[:, 128:160]
+        tt(AG, T.UU[:], T.GG[:], mul, ["U0", "U1", "GG0", "GG1"], ["AG"])
+        tt(T.pK[:], T.wa[:, 0:32], T.pKc[:], add, ["wa", "pKc0", "pKc1"], ["pK"])
+        tt(CH, T.UU[:], AG, sub, ["U0", "U1", "AG"], ["CH"])
+        tt(P[:, 0:32], AG, T.pK[:], mul, ["AG", "pK"], ["Pa"])
+        tt(P[:, 64:96], AG, T.TT[:], mul, ["AG", "TT"], ["Pe"])
+        tt(P[:, 32:64], CH, T.tD[:], mul, ["CH", "tD0", "tD1"], ["Pb"])
+        cp(T.au[:], T.wa[:, 33::2], ["wa"], ["au"])
+        tt(R[:, 32:112], P[:, 0::2], P[:, 1::2], add, ["Pa", "Pb", "Pe", "AG", "CH"], ["R"])
+        tt(R[:, 0:16], R[:, 80:96], T.dE[:], mul, ["R", "dE"], ["Ra"])
+        tt(R[:, 16:32], R[:, 96:112], R[:, 80:96], sub, ["R"], ["Rb"])
+        tt(T.LF[:], R[:, 0:64], T.BASE[:], add, ["R", "Ra", "Rb", "B0", "B1", "B2", "B3"], ["LF"])
+        cp(T.LU[:], T.LF[:], ["LF"], ["LU"])
+
+        S = T["S%d" % (r % 2)]
+        sk = "S%d" % (r % 2)
+        act(T.G2[:], Dm[:].indirect(T.LU[:, 0:16]), AF.Abs, ["Dm%d" % h for h in range(NB)] + ["zb", "zh", "LU"], ["G2"],
+            scale=2.0)
+        tt(T.v2[:], W[:].indirect(T.LU[:, 32:48]), T.G2[:], add, ["Wk%d" % u for u in range(8)] + ["W0", "LU", "G2"], ["v2"])
+        ts(S[:, :, 64:128], T.v2[:], -0.5, 0.5, add, mul, ["v2"], [sk + "z"])
+        cp(T.zn[:], S[:, :, 64:128], [sk + "z"], ["zn"])
+        for b in range(16):
+            mm(bk(4, 256, 272), T.ZU[:, 15 - b:143 - b], T.zn[:, b::16], b == 0, b == 15, ["ZU", "zn"], ["uL"], [4])
+        ts(T.nMi[:], T.QW[:].indirect(T.LU[:, 16:32]), 4095, None, band, None, ["QA", "QB", "Mi", "LU"], ["nMi"])
+        cp(T.ui[:], bk(4, 256, 272), ["uL"], ["ui"], [4])
+        if not last:
+            aff(T.nag[:], R[:, 80:96], -1.0, 1.0, ["R"], ["nag"])
+            cp(S[:, :, 0:64], T.nMi[:], ["nMi"], [sk + "m"])
+            tt(T.c1[:], T.ui[:], T.nag[:], mul, ["ui", "nag"], ["c1"])
+            tt(T.ci[:], T.c1[:], R[:, 64:80], add, ["c1", "R"], ["ci"])
+            ts(T.cn[:], T.ci[:], 1023, None, band, None, ["ci"], ["cn"])
+            cp(S[:, :, 128:132], T.cn[:], ["cn"], [sk + "c"])
+            Ln = T["L%d" % (r + 1)]
+            SK = [sk + "m", sk + "z", sk + "c", sk + "p"]
+
+            def travel(S=S, Ln=Ln, r=r):
+                tr = []
+                for h in range(1, n):
+                    d = dsts[h - 1]
+                    rid, pid, _ = topo.addr(d)
+                    tr.append(RemoteDMATransfer(dst_ids=[DstId(rid=rid, pnc=pid)],
+                                                dma_engine_mask=sum(1 << e for e in eng[d]),
+                                                remote_sem=T.sem["arr%d" % r],
+                                                src=S[:, h, :], dst=Ln[:, (h + 1) % n, :]))
+                g.remote_dma_fused(tr, local_sem=T.sem["snt%d" % r])
+
+            op("g", travel, SK, ["snt%d" % r], sem=("snt%d" % r, sum(len(eng[d]) for d in dsts)))
+            op("g", None, ["snt%d" % r], ["arr"], sem=("arr%d" % r, arrivals))
+            cp(Ln[:, 1, :], S[:, 0, :], SK, ["Lown"])
+
+        ts(T.u15[:], T.ui[:], 15, None, band, None, ["ui"], ["u15"])
+        tt(T.vf[:], T.u15[:], T.c16[:], add, ["u15", "c16"], ["vf"])
+        cp(T.vu[:], T.vf[:], ["vf"], ["vu"])
+        tt(T.sx[:], X[:].indirect(T.vu[:]), T.zn[:], add, ["X", "vu", "zn"], ["sx"])
+        ts(T.sxu[:], T.sx[:], -0.5, 0.5, add, mul, ["sx"], ["sxu"])
+        cp(X[:].indirect(T.vu[:]), T.sxu[:], ["vu", "sxu"], ["X"])
+
+        aff(T.eE[:], T.E[:, 0:16].indirect(T.eu[:]), 1.0, 0.0, ["E", "eu"], ["eE"])
+        aff(bk(4), T.eE[:], 1.0, 0.0, ["eE"], ["p44"], [4])
+        tt(T.Xn[:], bk(4), Mi, mul, ["p44", "Mi"], ["Xn"], [4])
+        tt(T.nb[:], T.LF[:, 48:64], T.i256[:], add, ["LF", "i256"], ["nb"])
+        tt(T.krep[:], T.tab[:].indirect(T.LU[:, 48:64]), T.iF[:], add, ["tab", "LU", "iF"], ["krep"])
+        for a in range(16):
+            for j in range(2):
+                lo, hi = 64 * (a // 4), 16 * (a + 1)
+                c = 16 * j + a
+                act(T.junk[:, 64 * c:64 * c + hi - lo], T.krep[:, lo:hi], AF.Sign, ["krep", "nb", "LF"], ["s%d" % c],
+                    scale=-1.0, bias=T.LF[:, 48 + a:49 + a] if j else T.nb[:, a:a + 1], acc=T.s12[:, c:c + 1])
+        aff(T.old[:], K[:].indirect(T.LU[:, 48:64]), 1.0, 0.0, ["K", "Kd", "LU"], ["old"])
+        aff(T.eA[:], T.E[:, 16:32].indirect(T.au[:]), 1.0, 0.0, ["E", "au"], ["eA"])
+        mm(bk(5), T.Bf[:], T.Xn[:], True, False, ["Bf", "Xn"], ["p45"], [5])
+        mm(bk(5), T.Inf[:], T.old[:], False, True, ["Inf", "old"], ["p45"], [5])
+        tt(T.Y[:], bk(5), T.eA[:], mul, ["p45", "eA"], ["Y"], [5])
+        tt(T.eq[:], T.s12[:, 0:16], T.s12[:, 16:32], ALU.is_equal, ["s%d" % c for c in range(32)], ["eq"])
+        tt(T.of1[:], T.eq[:], R[:, 48:64], mul, ["eq", "R"], ["of1"])
+        tt(T.of2[:], T.of1[:], T.BASE[:, 48:64], add, ["of1", "B3"], ["of2"])
+        cp(T.ofu[:], T.of2[:], ["of2"], ["ofu"])
+        for h in range(NB - 1, -1, -1):
+            tt(K[:].indirect(T.ofu[:, 4 * h:4 * h + 4]), T.old[:, 64 * h:64 * h + 64], T.Y[:, 64 * h:64 * h + 64], add,
+               ["ofu", "old", "Y"], ["K", "Kd"])
+
+        if last:
+            cp(T.nMf[:], T.nMi[:], ["nMi"], ["nMf"])
+            dma("s", T.yz[:], T.zn[:], ["zn"], ["yz"], "oz")
+            dma("s", T.ytx[:], X[:], ["X"], ["ytx"], "ox")
+            dma("s", T.ykt[:], K[:, 0:1024], ["K"], ["ykt"], "ok")
+            dma("s", T.yms[:], T.nMf[:], ["nMf"], ["yms"], "om")
+        else:
+            mm(bk(4, 256, 272), T.Bf[:], R[:, 96:112], True, True, ["Bf", "R"], ["uL"], [4])
+            act(T.aj[:], bk(4, 256, 272), AF.Identity, ["uL"], ["aj", "A128"], [4], scale=128.0, acc=T.Ac[:, 0:1])
+            aff(T.Ac[:, 1:2], T.Ac[:, 0:1], 1.0, 64.0, ["A128"], ["A64"])
+            aff(T.Ac[:, 2:3], T.Ac[:, 0:1], 1.0, -1.0, ["A128"], ["Am1"])
+            cp(zb, Ln[:, :, 64:128], ["arr", "Lown"], ["zb"])
+            cp(T.cu[:], Ln[:, :, 128:132], ["arr", "Lown"], ["cu"])
+            if len(FS) == 1:
+                spread(zb, ["zb"], 0, NB, FS[0])
+            else:
+                spread(T.zn[:, 0:64], ["zn"], 1, 1, FS[0])
+                spread(Dm[:, ZB:ZB + 64], ["zb"], 0, 1, FS[1])
+                spread(Dm[:, ZB + 128:ZB + 256], ["zb"], 2, 2, FS[2])
+    op("s", None, ["ytx", "ykt", "yz", "yms"], [])
+    op("g", None, ["snt0", "snt1"], [])
+    emit(g, T, ops[:loads] + [o for o in ordered(ops) if not (o["sem"] and o["sem"][0][:2] == "ld")])

@@ -2,14 +2,18 @@ from concourse.bass import DstId, RemoteDMATransfer
 from concourse.mybir import AluOpType as ALU, ActivationFunctionType as AF
 
 RO, NB, ROW = 3, 4, 136
-ZERO = 4096
-ZB, ZH = 4096, 4352
-N4 = [3, 4, 4]
-KORD = [2, 3, 0, 1, 4, 5, 6, 7]
-FS = [16, 16, 0]
-SAME = True
+SP = 64
 BIG = 1.0e6
-ORDER = "0004050602030<010@1H0A0H080F0L0M0I190E0G0N0K090J180C0B0D071>151L0=140;100>0W0:0O1M121R0P0?1W1U1=0R231@0S1J270T241K210U1?1Q0V113P16291:1P1;1S1B1C1V1A3?1O130Q25221I171T1N281<201D261E1F3O1G3R3W3V2<2=2;2@2G2W2J2H2B2A2K302D2>37382C2E2M2?3<3;2Q2N332L2O342I312S2F322R2U352P3N392V3M2:2T36413=4243443A3Q3S3U3:5746453@3>474;4:5849483C4<3B4=594>4A4?4@4B3D3T4D404F4P4E4C4G3G3E4H5:4I5;3F5V4J625L60635>4K5O5B5M4L5Q3J5?4M5P5<3H615U5G3K5T5E5A4O3I5D6@5=5K4R5J515@4S5N523L5I5R5C535S4N5W5F5H6L6K4T6P6I4Q6F6M6U546T6G6S6O6H6R4U6N556Q4V6J68645665666A696C506B6:7R4W677S6;6D6E7B6<7I6=747<8F6V7:7H706>797273767A758G6?7771787=7;7D7F8W7@7>7N7M7E827K927?7J7L7C7G9?8085836W84867T87818H8I7O7U7V8R888K7P8S7W9>8D898B8;8N8O8@8E8<8C8>8J8:8U8=9A7Q9=8?8T9F9@9E9B9<8A8L9C9D9G:N8P9H:O8Q9I9L9J9K909M8V8M9N:P939R919O9Q9P9S9T9U9V96:0949W:1:2:3;L95:597:?:498:6:7:Q:R;K99:8;M9:;A;0:9;=;6;4;I;5;F::;;9;;H;C;@:;;8:=;D:<:S;E;3:T;N:V;>;7:>;1:@;9;W;G;<:A:H;J:B;::I:U:C;?:J;B:D:K:W:E;2<7<C<><;;O<D:G<B:L<?<@;P<A:M<=<6<9<8<:<5<<<0<2<1;Q=A:FAC;R<3=B;S=0=:;T=<<W<E;U<G>5<I<S<P<V<H=1<J=3<K;V<O<L>6<M<T=8<N=4<Q=6<F==<R=2=;=I=5=9<U=7<4=E=L=J=K=M=C=F=N=>=D>7=G>==O>9=?=H=P>U>3=U=R>A>1>4=S=V>>=W>2=Q>C>V>S>T=T?0>W?5?3>0?4?2>;?1?6=@?7?8>??9?:>E>F>B?;@4?<>:?=@5?A?@???>?B>G?C?D?E?F>J?G?H?I?JA2?L?K>I?M?N@7?O@8>8>K?P@9@N>D@O@G?Q@K@:A1?R>N?SA>@L>O@W@?@M>@@;?U@S?V@E@H?W@VA0@0><@T@1@J@F@B@A@Q>H@2@3@<>L@U@@@>@C@P@R@I@=@D@6A?A5>PA3A6A7A8>MA4A9A:A;A<>Q>R?TA@A=AAAB"
+CFG = {
+    "parts": [(0, 16)],
+    "nb": ["aavaavav"] * 3,
+    "mord": [[0, 1, 2, 3], [1, 2, 3, 0], [1, 2, 3, 0]],
+    "zs": [(1, 1, "a" * 8 + "v" * 8), (2, 2, "v" * 16), (0, 1, "g" * 16)],
+    "kcu_a": True, "ku": 1,
+    "sg": [[(0, 1), (1, 1), (2, 1), (3, 1)]] * 2,
+    "kg": [[(0, 4)], [(0, 4)]], "cg": [[(0, 4)], [(0, 4)]],
+    "lat": 100.0, "passes": 8, "rem": 2600.0, "gam": 1.3, "f": 1.1,
+}
 
 
 def _sb(n, d):
@@ -18,38 +22,37 @@ def _sb(n, d):
 
 F, H, I, U, Q = "float32", "bfloat16", "int32", "uint16", "float16"
 SCRATCH = {
-    "X": _sb(4096, H), "W": _sb(4112, H), "Dm": _sb(4608, H), "zrep": _sb(4096, H),
-    "adM": _sb([16, 256], H), "adK": _sb([16, 256], H),
-    "kti": _sb(1024, I), "K": _sb(1280, F), "msi": _sb(256, I), "cpi": _sb(16, I),
+    "X": _sb(4096, H), "W": _sb(4160, H), "Dm": _sb(4096, H), "zrep": _sb(4096, H),
+    "AD": _sb(20 * 256, H), "adM": _sb([16, 256], H), "adK": _sb([16, 256], H),
+    "kti": _sb(1024, I), "K": _sb(SP + 1024, F), "K2": _sb(SP + 1024, F), "msi": _sb(256, I), "cpi": _sb(16, I),
     "L0": _sb([NB, ROW], U), "L1": _sb([NB, ROW], U), "L2": _sb([NB, ROW], U),
     "S0": _sb([NB, ROW], U), "S1": _sb([NB, ROW], U),
-    "QW": _sb(768, I), "kcu": _sb(256, U), "kc4": _sb(256, F), "km": _sb(256, F), "kk": _sb(256, F),
-    "P2s": _sb(256, F), "q1": _sb(256, F), "nMi": _sb(256, I), "nMf": _sb(256, F),
-    "G2": _sb(256, H), "v2": _sb(256, Q), "zn": _sb(256, H), "sx": _sb(256, Q), "sxu": _sb(256, U),
-    "krep": _sb(256, F), "eE": _sb(256, F), "Xn": _sb(256, F), "eA": _sb(256, F), "old": _sb(256, F), "Y": _sb(256, F),
-    "junk": _sb(2048, H), "s12": _sb(32, F), "nb": _sb(16, F),
-    "scm": _sb(256, I), "sct": _sb(256, F), "sck": _sb(512, I), "scs": _sb(256, F),
-    "cu": _sb(16, U), "c2": _sb(32, I), "TT": _sb(32, I), "tD": _sb(32, F),
-    "ei": _sb(16, I), "eu": _sb(16, U), "mt": _sb(16, F), "dE": _sb(16, F),
-    "aDT": _sb(16, F), "thP": _sb(16, F), "tm": _sb(16, F), "thN": _sb(16, F), "Ac": _sb(4, F), "aj": _sb(16, F),
-    "UU": _sb(32, F), "GG": _sb(32, F), "wa": _sb(64, I), "pK": _sb(32, F),
-    "P": _sb(160, F), "R": _sb(112, F), "BASE": _sb(64, F), "LF": _sb(64, F), "LU": _sb(64, U),
-    "au": _sb(16, U), "nag": _sb(16, F),
-    "ui": _sb(16, I), "u15": _sb(16, I), "vf": _sb(16, F), "vu": _sb(16, U),
-    "c1": _sb(16, F), "ci": _sb(16, I), "cn": _sb(16, I),
-    "eq": _sb(16, F), "of1": _sb(16, F), "of2": _sb(16, F), "ofu": _sb(16, U),
-    "ones": _sb(256, F), "pi": _sb(1, I), "fi": _sb(1, I), "col": _sb(8, F), "If": _sb(128, F), "Bt": _sb(128, F),
-    "Bf": _sb(128, F), "srow": _sb(128, F), "Ht": _sb(128, F), "Hm": _sb(128, F), "P2m": _sb(128, F), "t2": _sb(128, F),
-    "Ip": _sb(128, F), "In": _sb(128, F), "Inf": _sb(128, F),
-    "Ib": _sb(128, H), "Inb": _sb(128, H), "I37": _sb(128, H), "Ub": _sb(128, H),
-    "Z": _sb(144, H), "ZU": _sb(144, H), "ktab": _sb(128, H), "kcol": _sb(256, H),
-    "r16": _sb(256, F), "r8": _sb(256, F), "rx": _sb(256, F), "rs": _sb(256, F),
-    "Et": _sb(32, F), "E": _sb(32, F), "tab": _sb(1280, F), "iF": _sb(256, F), "i0": _sb(16, F), "iL": _sb(16, F),
-    "c16": _sb(16, F), "pKc": _sb(32, F), "zp": _sb(48, F), "i256": _sb(16, F),
+    "QW": _sb(768, F), "Mf": _sb(256, F), "kcu": _sb(256, U), "kcq": _sb(256, Q), "km": _sb([2, 8, 32], Q), "tr": _sb([2, 8, 32], Q),
+    "sg": _sb([3, 8, 32], H), "MP": _sb([6, 160], H), "cx": _sb(16, F), "nM": _sb(256, I), "nMi": _sb(256, I), "nMf": _sb(256, F),
+    "Hh": _sb(256, F), "zn": _sb(256, Q), "znb": _sb(256, H), "o2": _sb(256, F), "sx": _sb(256, I),
+    "Xn": _sb(256, F), "eA": _sb(256, F), "old": _sb(256, F), "Y": _sb(256, F),
+    "aD": _sb(1024, H), "kp": _sb(1024, H), "tf": _sb(16, Q), "kb": _sb(16, F), "fl": _sb(16, F),
+    "scm": _sb(256, I), "sct": _sb(256, F), "sck": _sb([2, 256], I), "scs": _sb(256, F),
+    "cu": _sb(16, U), "c5": _sb(16, F), "c5i": _sb(16, I), "TT": _sb(32, F), "TD": _sb(32, F),
+    "ei": _sb(16, I), "eu": _sb(16, U),
+    "aDT": _sb(16, F), "thP": _sb(16, F), "tm": _sb(16, F), "thN": _sb(16, F), "Ac": _sb(4, F), "aj": _sb(32, F),
+    "UU": _sb(32, F), "GG": _sb(32, F), "AG": _sb(32, F), "CH": _sb(32, F), "wa": _sb([2, 32], I), "pK": _sb(32, F),
+    "P": _sb([5, 32], F), "R": _sb([5, 16], F), "BASE": _sb([4, 16], F), "LF": _sb([4, 16], F), "LU": _sb([4, 16], U),
+    "au": _sb(16, U), "ui": _sb(16, I), "u15": _sb(16, I), "vf": _sb(16, F), "vu": _sb(16, U),
+    "ci": _sb(16, I), "cn": _sb([NB, 2, 4], I), "of1": _sb(16, F), "of2": _sb(16, F), "ofu": _sb(16, U),
+    "ones": _sb(256, F), "oneb": _sb(256, H), "pi": _sb(1, I), "fi": _sb(1, I), "col": _sb(8, F), "If": _sb(128, F),
+    "Bt": _sb(128, F), "Bf": _sb(128, F), "Bb": _sb(128, H), "srow": _sb(128, F), "Ht": _sb(128, F), "Hm": _sb(128, H),
+    "P2m": _sb(128, H), "t2": _sb(128, F), "Inf": _sb(128, F), "Ih": _sb(128, H), "I13": _sb(128, H), "I17": _sb(128, H),
+    "Ib": _sb(128, H), "Inb": _sb(128, H), "I37": _sb(128, Q), "Ub": _sb(128, H), "I7": _sb(128, H),
+    "DL": _sb([16, 128], H), "Z": _sb(144, H), "ZU": _sb(144, H), "I4": _sb(128, H), "jl": _sb(256, H),
+    "r16": _sb(256, F), "r8": _sb(256, F), "rx": _sb(256, F), "rs": _sb(256, F), "r1": _sb(1024, H),
+    "Et": _sb(32, F), "E": _sb(32, F), "i0": _sb(32, F), "iL": _sb(16, F),
+    "cw": _sb(16, F), "pKc": _sb(32, F), "zp": _sb(32, F), "kc": _sb(16, F),
     "ps": ("psum", [128, 4096], F),
 }
-SEMAPHORES = ["v", "a", "p", "g", "ldx", "ldk", "ldm", "ldz", "ldc", "arr0", "arr1", "snt0", "snt1",
-              "ox", "ok", "om", "oz"]
+SEMAPHORES = ["v", "a", "p", "g", "ldx", "ldk", "ldm", "ldz0", "ldz1", "ldc", "arr0", "arr1", "snt0", "snt1", "k2",
+              "ox0", "ox1", "ok", "om0", "om1", "oz0", "oz1"]
+SEMAPHORES += ["ad%d_%d" % (r, h) for r in range(RO) for h in range(NB)]
 
 
 def engine_split(topo, src, dsts):
@@ -69,10 +72,61 @@ def engine_split(topo, src, dsts):
     return res
 
 
-def ordered(ops):
-    if len(ORDER) != 2 * len(ops):
-        return ops
-    return [ops[(ord(ORDER[j]) - 48) * 40 + ord(ORDER[j + 1]) - 48] for j in range(0, len(ORDER), 2)]
+def schedule(ops):
+    lat, n = CFG["lat"], len(ops)
+    pred, succ = [set() for _ in ops], [[] for _ in ops]
+    last_w, readers = {}, {}
+    for j, o in enumerate(ops):
+        for k in o["r"] + o["w"]:
+            if k in last_w:
+                pred[j].add(last_w[k])
+        for k in o["w"]:
+            pred[j].update(readers.get(k, []))
+        pred[j].discard(j)
+        for k in o["r"]:
+            readers.setdefault(k, []).append(j)
+        for k in o["w"]:
+            last_w[k] = j
+            readers[k] = []
+        for m in pred[j]:
+            succ[m].append(j)
+
+    def gap(m, s):
+        return ops[m]["d"] + (0.0 if ops[m]["e"] == "p" and ops[s]["e"] == "p" else lat)
+
+    def place(seq, before, back):
+        start, busy = [0.0] * n, {}
+        for j in seq:
+            o = ops[j]
+            s = max([start[m] + ops[m]["t"] + (gap(j, m) if back else gap(m, j)) for m in before[j]] + [o["d"] if back else 0.0])
+            t = o["t"]
+            taken = [v for v in busy.get(o["e"], []) if v[1] > s]
+            for b in o["b"]:
+                taken += [(x - lat, y + lat) for x, y, f in busy.get(b, []) if f != o["e"] and y + lat > s]
+            for x in sorted(taken):
+                if s + t <= x[0]:
+                    break
+                s = max(s, x[1])
+            start[j] = s
+            busy.setdefault(o["e"], []).append((s, s + t))
+            for b in o["b"]:
+                busy.setdefault(b, []).append((s, s + t, o["e"]))
+        return start
+
+    way = [0.0] * n
+    for j in range(n - 1, -1, -1):
+        way[j] = ops[j]["t"] + max([gap(j, s) + way[s] for s in succ[j]] + [ops[j]["d"]])
+    seq = sorted(range(n), key=lambda j: (-way[j], j))
+    best = None
+    for _ in range(CFG["passes"]):
+        start = place(seq, pred, False)
+        end = max(start[j] + ops[j]["t"] + ops[j]["d"] for j in range(n))
+        if best is None or end < best[0]:
+            best = (end, start)
+        rev = place(sorted(range(n), key=lambda j: (-start[j] - ops[j]["t"], -j)), succ, True)
+        seq = sorted(range(n), key=lambda j: (-rev[j] - ops[j]["t"], j))
+    CFG["end"] = best[0]
+    return sorted(range(n), key=lambda j: (best[1][j], j))
 
 
 def emit(g, T, ops):
@@ -82,22 +136,19 @@ def emit(g, T, ops):
     done, waits, marked = [], [], set()
     for n, o in enumerate(ops):
         e = o["e"]
-        if o["f"] is None and o["sem"]:
+        if e == "x":
             waits.append([])
             done.append({o["sem"][0]: n})
             for k in o["w"]:
                 last_w[k] = n
                 readers[k] = []
             continue
-        deps, over = set(), set()
-        for k in o["r"]:
+        deps = set()
+        for k in o["r"] + o["w"]:
             if k in last_w:
                 deps.add(last_w[k])
         for k in o["w"]:
-            if k in last_w:
-                over.add(last_w[k])
-            over.update(readers.get(k, []))
-        deps.update(m for m in over if SAME or ops[m]["e"] != e or ops[m]["sem"] or o["sem"])
+            deps.update(readers.get(k, []))
         for b in o["b"]:
             deps.update(m for f, m in bank.get(b, {}).items() if f != e)
         ws = []
@@ -154,136 +205,160 @@ def rank_program(g, core, T, topo):
     V, A, PE = g.vector, g.scalar, g.tensor
     ops = []
 
-    def op(e, f, r, w, b=(), sem=None):
-        ops.append({"e": e, "f": f, "r": list(r), "w": list(w), "b": list(b), "sem": sem})
+    def op(e, f, r, w, t, b=(), sem=None, d=0.0):
+        ops.append({"e": e, "f": f, "r": list(r), "w": list(w), "b": list(b), "sem": sem, "t": t, "d": d})
 
-    def cp(out, in_, r, w, b=()):
-        op("v", lambda: V.tensor_copy(out, in_), r, w, b)
+    def ns(c):
+        if isinstance(c, tuple):
+            return 55.0 + max(64, c[1]) * (CFG["gam"] if c[0] == "g" else 3.2)
+        return CFG["f"] * 0.83 * max(64, c)
 
-    def tt(out, a, c, o, r, w, b=()):
-        op("v", lambda: V.tensor_tensor(out, a, c, o), r, w, b)
+    def cp(out, in_, r, w, c=0, b=()):
+        op("v", lambda: V.tensor_copy(out, in_), r, w, ns(c), b)
 
-    def ts(out, a, s1, s2, o0, o1, r, w, b=()):
+    def tt(out, a, c_, o, r, w, c=0, b=()):
+        op("v", lambda: V.tensor_tensor(out, a, c_, o), r, w, ns(c), b)
+
+    def ts(out, a, s1, s2, o0, o1, r, w, c=0, b=()):
         if s2 is None:
-            op("v", lambda: V.tensor_scalar(out, a, s1, None, o0), r, w, b)
+            op("v", lambda: V.tensor_scalar(out, a, s1, None, o0), r, w, ns(c), b)
         else:
-            op("v", lambda: V.tensor_scalar(out, a, s1, s2, o0, o1), r, w, b)
+            op("v", lambda: V.tensor_scalar(out, a, s1, s2, o0, o1), r, w, ns(c), b)
 
-    def ms(out, c, w):
-        op("v", lambda: V.memset(out, c), [], w)
+    def ms(out, x, w, c=0):
+        op("v", lambda: V.memset(out, x), [], w, ns(c))
 
-    def scan(out, d0, d1, o0, o1, r, w, b):
-        op("v", lambda: V.tensor_tensor_scan(out, d0, d1, 0.0, o0, o1), r, w, b)
+    def scan(out, d0, d1, o0, o1, r, w, c, b=()):
+        op("v", lambda: V.tensor_tensor_scan(out, d0, d1, 0.0, o0, o1), r, w, ns(c), b)
 
-    def act(out, in_, fn, r, w, b=(), bias=0.0, scale=1.0, acc=None):
-        op("a", lambda: A.activation(out, in_, fn, bias=bias, scale=scale, accum_out=acc), r, w, b)
+    def act(out, in_, fn, r, w, c=0, b=(), bias=0.0, scale=1.0, acc=None):
+        op("a", lambda: A.activation(out, in_, fn, bias=bias, scale=scale, accum_out=acc), r, w, ns(c), b)
 
-    def aff(out, in_, scale, bias, r, w, b=()):
-        act(out, in_, AF.Identity, r, w, b, bias=bias, scale=scale)
+    def aff(out, in_, scale, bias, r, w, c=0, b=()):
+        act(out, in_, AF.Identity, r, w, c, b, bias=bias, scale=scale)
 
-    group = []
+    def mm(out, terms, r, w, b, c):
+        def run():
+            for j, m in enumerate(terms):
+                ins = PE.matmul(m[2] if len(m) > 2 else out, m[0], m[1], j == 0, j == len(terms) - 1)
+            return ins
+        op("p", run, r, w, CFG["f"] * 0.42 * c, [b])
 
-    def mm(out, l, rh, st, sp, r, w, b):
-        group.append((out, l, rh, st, sp, r))
-        if sp:
-            part = list(group)
-            del group[:]
-
-            def run():
-                for m in part:
-                    ins = PE.matmul(*m[:5])
-                return ins
-            op("p", run, [k for m in part for k in m[5]], w, b)
-
-    def iota(out, pat, base, cm, w, small=True):
+    def iota(out, pat, base, cm, w, c, small=True):
         if small:
-            op("g", lambda: g.iota(out, pat, base, cm, allow_small_or_imprecise_dtypes=True), [], w)
+            op("g", lambda: g.iota(out, pat, base, cm, allow_small_or_imprecise_dtypes=True), [], w, 140 + 1.8 * c)
         else:
-            op("g", lambda: g.iota(out, pat, base, cm), [], w)
+            op("g", lambda: g.iota(out, pat, base, cm), [], w, 140 + 1.8 * c)
 
-    def asel(out, in_, pat, o, fill, base, cm, r, w):
-        op("g", lambda: g.affine_select(out, in_, pat, o, fill, base, cm), r, w)
+    def asel(out, in_, pat, o, fill, base, cm, r, w, c):
+        op("g", lambda: g.affine_select(out, in_, pat, o, fill, base, cm), r, w, 185 + 1.8 * c)
 
-    def dma(e, out, in_, r, w, sem):
+    def gcp(out, in_, r, w, c):
+        asel(out, in_, [[0, c]], ALU.is_gt, 0.0, 1, 0, r, w, c)
+
+    def dma(e, out, in_, r, w, sem, d):
         qq = g.sync if e == "s" else g.scalar
-        op(e, lambda: qq.dma_start(out, in_), r, w, sem=(sem, 16))
+        op(e, lambda: qq.dma_start(out, in_), r, w, 50.0, sem=(sem, 16), d=d)
 
     def bk(b, a=0, c=256):
         return T.ps[:, 512 * b + a:512 * b + c]
 
-    W, X, K, Dm = T.W, T.X, T.K, T.Dm
-    zb = Dm[:, ZB:ZB + 256]
+    def ks(name, hs):
+        return ["%s%d" % (name, h) for h in hs]
+
+    W, X, K, Dm, AD = T.W, T.X, T.K, T.Dm, T.AD
     add, sub, mul, mx, mn = ALU.add, ALU.subtract, ALU.mult, ALU.max, ALU.min
     band = ALU.bitwise_and
     ones, col = T.ones, T.col
+    blocks = list(range(NB))
+    parts = CFG["parts"]
+    home = {}
+    for j, (a0, a1) in enumerate(sorted(parts)):
+        for h in range(a0 // 4, a1 // 4):
+            home[h] = (a0, a1, 256 * (a0 + j), 256 * a0 + 16 * j)
 
-    dma("a", zb, T.z[:], [], ["zb"], "ldz")
-    dma("a", T.msi[:], T.ms[:], [], ["msi"], "ldm")
-    dma("a", T.cpi[:], T.cp[:], [], ["cpi"], "ldc")
-    dma("s", X[:], T.tx[:], [], ["X"], "ldx")
-    dma("s", T.kti[:], T.kt[:], [], ["kti"], "ldk")
+    def zat(h, m):
+        a0, a1, ad0, _ = home[h]
+        c = ad0 + 256 * (a1 - a0) + 64 * h - 16 * a0
+        return AD[:, c:c + 64 * m]
+
+    for j, (a0, a1) in enumerate(parts):
+        dma("a", zat(a0 // 4, (a1 - a0) // 4), T.z[:, 16 * a0:16 * a1], [], ks("zb", range(a0 // 4, a1 // 4)), "ldz%d" % j, 1700)
+    dma("s", T.msi[:], T.ms[:], [], ["msi"], "ldm", 2200)
+    dma("a", T.cpi[:], T.cp[:], [], ["cpi"], "ldc", 2400)
+    dma("s", X[:], T.tx[:], [], ks("X", blocks), "ldx", 5400)
+    dma("s", T.kti[:], T.kt[:], [], ["kti"], "ldk", 7000)
     loads = len(ops)
 
-    ms(ones[:], 1.0, ["ones"])
-    iota(T.pi[:], [[0, 1]], 0, 1, ["pi"], False)
-    asel(T.If[:], ones[:, 0:128], [[-1, 128]], ALU.is_equal, 0.0, 0, 1, ["ones"], ["If"])
-    asel(T.Bt[:], ones[:, 0:128], [[16, 8], [0, 16]], ALU.is_ge, 0.0, 15, -1, ["ones"], ["Bt"])
-    asel(T.Bf[:], T.Bt[:], [[-16, 8], [0, 16]], ALU.is_ge, 0.0, 0, 1, ["Bt"], ["Bf"])
-    iota(T.ktab[:], [[16, 2], [0, 4], [1, 16]], 0, 0, ["ktab"])
-    iota(T.i0[:], [[16, 16]], 0, 0, ["i0"])
-    iota(T.srow[:], [[0, 8], [-2, 2], [0, 8]], 1, 0, ["srow"])
-    iota(T.Et[:, 0:16], [[1, 16]], 0, 0, ["Et0"])
-    iota(T.Et[:, 16:31], [[-1, 15]], 14, 0, ["Et1"])
-    iota(T.tab[:], [[1, 1280]], 0, 0, ["tab"])
+    ms(ones[:], 1.0, ["ones"], 256)
+    ms(T.oneb[:], 1.0, ["oneb"], 128)
+    iota(T.pi[:], [[0, 1]], 0, 1, ["pi"], 1, False)
+    asel(T.If[:], ones[:, 0:128], [[-1, 128]], ALU.is_equal, 0.0, 0, 1, ["ones"], ["If"], 128)
+    asel(T.Bt[:], ones[:, 0:128], [[16, 8], [0, 16]], ALU.is_ge, 0.0, 15, -1, ["ones"], ["Bt"], 128)
+    asel(T.Bf[:], T.Bt[:], [[-16, 8], [0, 16]], ALU.is_ge, 0.0, 0, 1, ["Bt"], ["Bf"], 128)
+    iota(T.jl[:], [[0, 4], [1, 64]], 0, 0, ["jl"], 256)
+    iota(T.i0[:, 0:16], [[16, 16]], 0, 0, ["i0"], 16)
+    iota(T.i0[:, 16:32], [[0, 4], [16, 4]], 0, 0, ["i1"], 16)
+    iota(T.srow[:], [[0, 8], [-2, 2], [0, 8]], 1, 0, ["srow"], 128)
+    iota(T.Et[:, 0:16], [[-1, 16]], 15, 0, ["Et0"], 16)
+    iota(T.Et[:, 17:32], [[1, 15]], 0, 0, ["Et1"], 15)
+    ms(T.Et[:, 16:17], 15.0, ["Et2"])
+    ms(T.MP[:, :, 0:16], 0.0, ["MPp"])
+    ms(T.MP[:, :, 144:160], 0.0, ["MPp"])
     ms(T.Z[:], 0.0, ["Z"])
     ms(T.ZU[:], 0.0, ["ZU"])
-    ms(W[:, ZERO:ZERO + 16], 0.0, ["W0"])
-    ms(T.S0[:, :, 132:136], 0, ["S0p"])
-    ms(T.S1[:, :, 132:136], 0, ["S1p"])
-    ms(T.Et[:, 31:32], 15.0, ["Et2"])
-    ms(T.Ac[:, 1:2], 64.0, ["A64"])
-    ms(T.Ac[:, 2:3], -1.0, ["Am1"])
+    ms(T.Ac[:], 0.0, ["A"])
+    ms(T.K[:, 0:SP], 0.0, ["Kd"])
+    ms(T.BASE[:, 1, :], 0.0, ["B1"])
+    ms(T.r1[:], 0.0, ["r1"], 512)
+    ms(T.r1[:, 0::64], 1.0, ["r1"])
     ts(T.fi[:], T.pi[:], 15, None, band, None, ["pi"], ["fi"])
-    ms(T.BASE[:, 32:48], float(ZERO), ["B2"])
     cp(col[:, 0:1], T.fi[:], ["fi"], ["c0"])
-    ts(col[:, 1:2], T.fi[:], 2.0, 1.0, mul, add, ["fi"], ["c1_"])
+    aff(col[:, 1:2], col[:, 0:1], 2.0, 1.0, ["c0"], ["c1_"])
     ts(col[:, 2:3], T.fi[:], 7.5, 2.0, ALU.is_gt, mul, ["fi"], ["c2_"])
-    for buf, c in ((T.r16, 0.0), (T.r8, 0.0), (T.rx, 2.0), (T.rs, 1.0)):
-        aff(buf[:], ones[:], c, 0.0, ["ones"], ["rr"])
-    aff(K[:, 1024:1280], ones[:], 0.0, 0.0, ["ones"], ["Kd"])
-    for o_, k_, c in ((T.r16[:, 0::16], 16, BIG), (T.r8[:, 0::8], 32, BIG), (T.rx[:, 0::16], 16, -BIG),
-                      (T.rs[:, 0::16], 16, 0.0), (T.rs[:, 8::16], 16, -1.0)):
+    aff(col[:, 3:4], col[:, 0:1], 37.0, 0.0, ["c0"], ["c3_"])
+    aff(col[:, 4:5], col[:, 2:3], -1.0, 1.0, ["c2_"], ["c4_"])
+    aff(col[:, 5:6], col[:, 2:3], -0.5, 0.5, ["c2_"], ["c5_"])
+    for buf, c in ((T.r16, 1.0), (T.r8, 1.0), (T.rx, -1.0), (T.rs, 1.0)):
+        aff(buf[:], ones[:], c, 0.0, ["ones"], ["rr"], 256)
+    for o_, k_, c in ((T.r16[:, 0::16], 16, -BIG), (T.r8[:, 0::8], 32, -BIG), (T.rx[:, 0::16], 16, BIG), (T.rs[:, 0::16], 16, 0.0), (T.rs[:, 8::16], 16, -1.0)):
         aff(o_, ones[:, 0:k_], c, 0.0, ["ones", "rr"], ["rr"])
-    aff(T.Ib[:], T.If[:], 1.0, 0.0, ["If"], ["Ib"])
-    aff(T.Inb[:], T.If[:], -1.0, 0.0, ["If"], ["Inb"])
-    aff(T.I37[:], T.If[:], 37.0, 0.0, ["If"], ["I37"])
-    aff(T.Z[:, 15:128:16], T.Bf[:, 0::16], 16.0, 0.0, ["Bf", "Z"], ["Z"])
+    aff(T.QW[:, 1::3], ones[:], -1.0, 0.0, ["ones"], ["QC"], 256)
+    for name, c in (("Ib", 1.0), ("Inb", -1.0), ("Inf", -1.0), ("Ih", 0.5), ("I13", 8192.0), ("I17", 2.0 ** 17), ("I7", 1.0 / 128),
+                    ("I4", 16.0)):
+        aff(T[name][:], T.If[:], c, 0.0, ["If"], [name], 128)
+    aff(T.I37[:], T.If[:], col[:, 3:4], 0.0, ["If", "c3_"], ["I37"], 128)
+    aff(T.Z[:, 15:128:16], T.Bf[:, 0::16], -32.0, 0.0, ["Bf", "Z"], ["Z"])
     aff(T.ZU[:, 15:128:16], T.Bf[:, 0::16], col[:, 1:2], 0.0, ["Bf", "ZU", "c1_"], ["ZU"])
-    aff(T.Ub[:], T.Bf[:], col[:, 1:2], 0.0, ["Bf", "c1_"], ["Ub"])
-    aff(T.kcol[:], ones[:], col[:, 0:1], 0.0, ["ones", "c0"], ["kcol"])
-    aff(T.t2[:], T.Bf[:], -2.0 ** 17, 0.0, ["Bf"], ["t2"])
-    asel(T.P2m[:], T.t2[:], [[-1, 128]], ALU.not_equal, 15 * 2.0 ** 17, 0, 1, ["t2"], ["P2m"])
-    ts(col[:, 3:4], col[:, 2:3], -1.0, 1.0 / 32, add, mul, ["c2_"], ["c3_"])
-    ts(col[:, 4:5], col[:, 2:3], -1.0, 16384.0, add, mul, ["c2_"], ["c4_"])
-    aff(T.Ip[:], T.If[:], 16384.0, 0.0, ["If"], ["Ip"])
-    aff(T.In[:], T.If[:], -16384.0, 0.0, ["If"], ["In"])
-    aff(T.Inf[:], T.If[:], -1.0, 0.0, ["If"], ["Inf"])
-    aff(T.iL[:], T.i0[:], 1.0, col[:, 0:1], ["i0", "c0"], ["iL"])
-    aff(T.Ht[:], T.Bf[:], col[:, 4:5], 0.0, ["Bf", "c4_"], ["Ht"])
-    aff(T.c16[:], T.iL[:], 16.0, 0.0, ["iL"], ["c16"])
-    aff(T.BASE[:, 48:64], T.iL[:], 1.0, 1024.0, ["iL"], ["B3"])
-    aff(T.BASE[:, 16:32], T.iL[:], 3.0, 1.0, ["iL"], ["B1"])
-    for r in range(RO):
-        a4 = 2 * N4[r]
-        aff(T.zp[:, 16 * r:16 * r + a4], T.iL[:, 0:a4], 1.0, float(ZH), ["iL"], ["zpa%d" % r])
-        aff(T.zp[:, 16 * r + a4:16 * r + 16], T.iL[:, a4:16], 1.0, float(ZB), ["iL"], ["zpb%d" % r])
-    aff(Dm[:, ZH:ZH + 256], ones[:], 0.0, 0.0, ["ones"], ["zh"])
-    aff(T.i256[:], T.iL[:], 1.0 / 256, 0.0, ["iL"], ["i256"])
-    for h in range(2):
-        aff(T.pKc[:, h::2], T.iL[:], 16.0, -float(ZERO), ["iL"], ["pKc%d" % h])
-    tt(T.Hm[:], T.Ht[:], T.srow[:], mul, ["Ht", "srow"], ["Hm"])
+    aff(T.Ub[:], T.Bf[:], col[:, 1:2], 0.0, ["Bf", "c1_"], ["Ub"], 128)
+    aff(T.t2[:], T.Bf[:], -1.0, 0.0, ["Bf"], ["t2"], 128)
+    aff(T.Bb[:], T.Bf[:], 1.0, 0.0, ["Bf"], ["Bb"], 128)
+    asel(T.P2m[:], T.t2[:], [[-1, 128]], ALU.not_equal, 15.0, 0, 1, ["t2"], ["P2m"], 128)
+    aff(T.iL[:], T.i0[:, 0:16], 1.0, col[:, 0:1], ["i0", "c0"], ["iL"])
+    aff(T.BASE[:, 2, :], T.i0[:, 16:32], 1.0, col[:, 0:1], ["i1", "c0"], ["B2"])
+    aff(T.kc[:], T.BASE[:, 2, :], 1.0 / 128, -0.25, ["B2"], ["kc"])
+    aff(T.Ht[:], T.Bf[:], col[:, 4:5], 0.0, ["Bf", "c4_"], ["Ht"], 128)
+    for a0, a1 in parts:
+        iL, w0 = T.iL[:, a0:a1], home[a0 // 4][3]
+        ms(W[:, w0:w0 + 16], 0.0, ["W0"])
+        aff(T.cw[:, a0:a1], iL, 16.0, -256.0 * a0, ["iL"], ["cw"])
+        aff(T.cx[:, a0:a1], iL, 16.0, 15.0 - 256.0 * a0, ["iL"], ["cx"])
+        aff(T.BASE[:, 3, a0:a1], iL, 3.0, -48.0 * a0, ["iL"], ["B3"])
+        for h in range(2):
+            aff(T.zp[:, 2 * a0 + h:2 * a1:2], iL, 1.0, 256.0 * (a1 - a0) - 16.0 * a0, ["iL"], ["zp"])
+            aff(T.pKc[:, 2 * a0 + h:2 * a1:2], iL, 16.0, 8.0 * h + 23.0 - 256.0 * a0, ["iL"], ["pKc"])
+    tt(T.Hm[:], T.Ht[:], T.srow[:], mul, ["Ht", "srow"], ["Hm"], 256)
     ts(T.E[:], T.Et[:], col[:, 0:1], None, ALU.is_equal, None, ["Et0", "Et1", "Et2", "c0"], ["E"])
-    aff(T.iF[:], T.tab[:, 0:256], 1.0 / 256, 1.0 / 512, ["tab"], ["iF"])
+    for j in range(16):
+        ts(T.DL[:, j, :], T.Bb[:], T.E[:, 15 - j:16 - j], None, mul, None, ["Bb", "E"], ["DL%d" % j])
+    for mp, (src, name) in enumerate(((T.P2m, "P2m"), (T.Ib, "Ib"), (T.Hm, "Hm"))):
+        for a2 in range(2):
+            asel(T.MP[:, 2 * mp + a2, 16:144], src[:], [[0, 4], [1, 2], [0, 16]], ALU.is_equal, 0.0, -a2, 0, [name],
+                 ["MP%d" % (2 * mp + a2)], 128)
+
+    def groups(spec, hs):
+        cut = [(max(h, hs[0]), min(h + m, hs[-1] + 1)) for h, m in spec]
+        return [(x, y - x) for x, y in cut if y > x]
 
     dsts = [cores[(rank + h) % n] for h in range(1, n)]
     eng = engine_split(topo, core, dsts)
@@ -292,218 +367,291 @@ def rank_program(g, core, T, topo):
         s = (rank - h) % n
         arrivals += len(engine_split(topo, cores[s], [cores[(s + j) % n] for j in range(1, n)])[core])
 
-    def spread(src, r, h, m, on):
+    def spread(h, m, who, src=None, r=None):
+        hs = list(range(h, h + m))
         for k in range(16):
-            o = T.zrep[:, 1024 * h + k:1024 * (h + m):16]
-            keys = ["zr%d_%d" % (j, k) for j in range(h, h + m)]
-            if k < on:
-                aff(o, src, 1.0, 0.0, r, keys)
+            o, w = T.zrep[:, 1024 * h + k:1024 * (h + m):16], ks("zr%d_" % k, hs)
+            if who[k] == "g":
+                gcp(o, zat(h, m), ks("zb", hs), w, 64 * m)
+            elif who[k] == "a":
+                aff(o, zat(h, m), 1.0, 0.0, ks("zb", hs), w, 64 * m)
+            elif src is None:
+                cp(o, zat(h, m), ks("zb", hs), w, 32 * m)
             else:
-                cp(o, src, r, keys)
+                cp(o, src, r, w, 32 * m)
 
     def zr(u, m=1):
         return T.zrep[:, 512 * u:512 * (u + m)]
 
     def zk(h):
-        return ["zr%d_%d" % (h, k) for k in range(16)]
+        return ["zr%d_%d" % (k, h) for k in range(16)]
 
-    Mi = T.QW[:, 2::3]
     P, R = T.P, T.R
+    XK = ks("X", blocks)
+    KW = K[:, SP:]
 
     for r in range(RO):
         last = r == RO - 1
         Lr = T["L%d" % r]
-        n4 = N4[r]
+        lk = ["Lm"] * NB if r == 0 else ["arr", "Lown", "arr", "arr"]
         if r == 0:
-            spread(zb, ["zb"], 0, NB, 0)
+            for a0, a1 in parts:
+                spread(a0 // 4, (a1 - a0) // 4, "v" * 16)
             cp(T.cu[:], T.cpi[:], ["cpi"], ["cu"])
-            cp(Lr[:, :, 0:64], T.msi[:], ["msi"], ["Lm"])
-            cp(Mi, T.msi[:], ["msi"], ["Mi"])
-            cp(K[:, 0:1024], T.kti[:], ["kti"], ["K"])
-            cp(T.kcu[:], T.kti[:].indirect(T.cu[:]), ["kti", "cu"], ["kcu%d" % h for h in range(NB)])
+            ts(T.c5i[:], T.cpi[:], 511, None, band, None, ["cpi"], ["c5i"])
+            cp(T.c5[:], T.c5i[:], ["c5i"], ["c5"])
+            cp(Lr[:, :, 0:64], T.msi[:], ["msi"], ["Lm"], 256)
+            gcp(T.Mf[:], T.msi[:], ["msi"], ks("Mf", blocks), 256)
+            gcp(KW, T.kti[:], ["kti"], ["K"], 1024)
         else:
-            cp(T.kcu[:, 64:128], K[:, 0:1024].indirect(Lr[:, 1, 128:132]), ["K", "Lown"], ["kcu1"])
-            cp(T.kcu[:, 0:64], K[:, 0:1024].indirect(Lr[:, 0, 128:132]), ["K", "arr"], ["kcu0"])
-            cp(T.kcu[:, 128:256], K[:, 0:1024].indirect(T.cu[:, 8:16]), ["K", "cu"], ["kcu2", "kcu3"])
-            cp(Mi, Lr[:, :, 0:64], ["arr", "Lown"], ["Mi"])
-
-        for h in (1, 0, 2, 3):
-            us = [2 * h, 2 * h + 1]
-            d = Dm[:, 1024 * h:1024 * h + 1024]
-            tt(d, X[:].indirect(Lr[:, h, 0:64]), zr(2 * h, 2), sub,
-               ["X", "Lm" if r == 0 else "Lown" if h == 1 else "arr"] + zk(h), ["Dm%d" % h])
-            act(T.adM[:, 4 * h:4 * h + 4, :], d, AF.Abs, ["Dm%d" % h], ["aM%d" % u for u in us])
-        for j in range(8):
-            u = KORD[j] if r else j
-            d = W[:, 512 * u:512 * u + 512]
-            o = T.adK[:, 2 * u:2 * u + 2, :]
-            x = X[:].indirect(T.kcu[:, 32 * u:32 * u + 32])
-            if u < n4:
-                b, bw = ((4, ["p44", "uL"]), (5, ["p45"]), (7, ["P1", "Hs"]))[j % 3]
-                aff(d, x, 1.0, 0.0, ["X", "kcu%d" % (u // 2)], ["Wk%d" % u])
-                mm(bk(b, 0, 512), T.Ib[:], d, True, False, ["Ib", "Wk%d" % u], bw, [b])
-                mm(bk(b, 0, 512), T.Inb[:], zr(u), False, True, ["Inb"] + zk(u // 2), bw, [b])
-                act(o, bk(b, 0, 512), AF.Abs, bw, ["aK%d" % u], [b])
-            else:
-                tt(d, x, zr(u), sub, ["X", "kcu%d" % (u // 2)] + zk(u // 2), ["Wk%d" % u])
-                act(o, d, AF.Abs, ["Wk%d" % u], ["aK%d" % u])
-        for h in (1, 0, 2, 3):
-            for t in range(2):
-                ad = T.adM if t == 0 else T.adK
-                rd = ["Z", "a%s%d" % ("MK"[t], 2 * h), "a%s%d" % ("MK"[t], 2 * h + 1)]
-                o = bk(t, 64 * h, 64 * h + 64)
-                mm(o, T.Ib[:], T.ktab[:, 64 - 64 * t:128 - 64 * t], True, False, ["Ib", "ktab"], [], [t])
-                for b in range(16):
-                    mm(o, T.Z[:, 15 - b:143 - b], ad[:, 4 * h:4 * h + 4, 16 * b:16 * b + 16], False, b == 15,
-                       rd, ["key%d_%d" % (t, h)], [t])
-                o = bk(2 + t, 64 * h, 64 * h + 64)
-                for k in range(16):
-                    mm(o, T.Z[:, 15 - k:143 - k], ad[:, 4 * h:4 * h + 4, k::16], k == 0, k == 15,
-                       rd, ["d%d_%d" % (t, h)], [2 + t])
-        KM, KK, DM, DK = (["%s_%d" % (x, h) for h in range(NB)] for x in ("key0", "key1", "d0", "d1"))
-
-        aff(Dm[:, ZH:ZH + 32 * n4], Dm[:, ZB:ZB + 32 * n4], 0.5, 0.0, ["zb"], ["zh"])
-        act(T.kc4[:], K[:, 0:1024].indirect(T.cu[:]), AF.Identity, ["K", "cu"], ["kc4"], bias=4096.0)
-        aff(T.km[:], bk(2), 1.0 / 16, -1.0 / 16, DM, ["km"], [2])
-        aff(T.kk[:], bk(3), 1.0 / 16, col[:, 3:4], DK + ["c3_"], ["kk"], [3])
-        mm(bk(6), T.Ub[:], zb, True, False, ["Ub", "zb"], ["fr"], [6])
-        mm(bk(6), T.I37[:], T.kcol[:], False, False, ["I37", "kcol"], ["fr"], [6])
-        mm(bk(6), T.If[:], T.kc4[:], False, True, ["If", "kc4"], ["fr"], [6])
-        mm(bk(6, 256, 512), T.P2m[:], T.km[:], True, True, ["P2m", "km"], ["P2"], [6])
-        aff(T.P2s[:], bk(6, 256, 512), 1.0, 0.0, ["P2"], ["P2s"], [6])
-        mm(bk(7), T.Ip[:], T.km[:], True, False, ["Ip", "km"], ["P1"], [7])
-        mm(bk(7), T.In[:], T.kk[:], False, True, ["In", "kk"], ["P1"], [7])
-        mm(bk(7, 256, 512), T.Hm[:], T.kk[:], True, True, ["Hm", "kk"], ["Hs"], [7])
-        tt(bk(6), bk(6), T.P2s[:], mn, ["P2s", "fr"], ["fr"], [6])
-        tt(T.QW[:, 1::3], bk(6), Mi, mx, ["fr", "Mi"], ["QB"], [6])
-        tt(T.q1[:], bk(7), T.kc4[:], mn, ["P1", "kc4"], ["q1"], [7])
-        tt(bk(7, 256, 512), bk(7, 256, 512), T.q1[:], mn, ["Hs", "q1"], ["Hs"], [7])
-        tt(T.QW[:, 0::3], bk(7, 256, 512), Mi, mx, ["Hs", "Mi"], ["QA"], [7])
-
-        scan(T.sct[:], T.rs[:], bk(0), mul, add, ["rr"] + KM, ["sct"], [0])
-        scan(T.scm[:], T.r16[:], bk(0), add, mn, ["rr"] + KM, ["scm"], [0])
-        for h in range(2):
-            ts(T.c2[:, h::2], T.cu[:], 2.0, float(h), mul, add, ["cu"], ["c2%d" % h])
-        ts(T.ei[:], T.scm[:, 15::16], 15, None, band, None, ["scm"], ["ei"])
-        ts(T.TT[:], T.c2[:], 1023, None, band, None, ["c20", "c21"], ["TT"])
-        cp(T.eu[:], T.ei[:], ["ei"], ["eu"])
-        tt(T.BASE[:, 0:16], T.ei[:], T.c16[:], add, ["ei", "c16"], ["B0"])
-        tt(T.mt[:], T.scm[:, 15::16], T.ei[:], sub, ["scm", "ei"], ["mt"])
-        for h in range(2):
-            tt(T.tD[:, h::2], T.TT[:, 1 - h::2], T.BASE[:, 48:64], sub, ["TT", "B3"], ["tD%d" % h])
-        tt(T.dE[:], T.zp[:, 16 * r:16 * r + 16], T.BASE[:, 0:16], sub, ["zpa%d" % r, "zpb%d" % r, "B0"], ["dE"])
-        act(T.aDT[:], T.sct[:, 15::16], AF.Abs, ["sct"], ["aDT"], bias=-64.0)
-        act(T.tm[:], T.aDT[:], AF.Relu, ["aDT", "Am1"], ["tm"], bias=T.Ac[:, 2:3])
-        aff(T.thP[:], T.aDT[:], 1.0, T.Ac[:, 1:2], ["aDT", "A64"], ["thP"])
-        aff(T.thN[:], T.tm[:], -1.0, 63.0, ["tm"], ["thN"])
-        scan(T.scs[:], T.rs[:], bk(1), mul, add, ["rr"] + KK, ["scs"], [1])
-        scan(T.sck[:, 0:256], T.r8[:], bk(1), add, mn, ["rr"] + KK, ["sck"], [1])
-        scan(T.sck[:, 256:512], T.rx[:], bk(1), add, mx, ["rr"] + KK, ["scx"], [1])
-        tt(T.UU[:, 0::2], T.scs[:, 15::16], T.thP[:], ALU.is_ge, ["scs", "thP"], ["U0"])
-        tt(T.UU[:, 1::2], T.scs[:, 15::16], T.thN[:], ALU.is_le, ["scs", "thN"], ["U1"])
-        for h in range(2):
-            tt(T.GG[:, h::2], T.sck[:, 7 + 8 * h:256:16], T.mt[:], ALU.is_lt, ["sck", "mt"], ["GG%d" % h])
-        ts(T.wa[:], T.sck[:, 7::8], 15, None, band, None, ["sck", "scx"], ["wa"])
-        AG, CH = P[:, 96:128], P[:, 128:160]
-        tt(AG, T.UU[:], T.GG[:], mul, ["U0", "U1", "GG0", "GG1"], ["AG"])
-        tt(T.pK[:], T.wa[:, 0:32], T.pKc[:], add, ["wa", "pKc0", "pKc1"], ["pK"])
-        tt(CH, T.UU[:], AG, sub, ["U0", "U1", "AG"], ["CH"])
-        tt(P[:, 0:32], AG, T.pK[:], mul, ["AG", "pK"], ["Pa"])
-        tt(P[:, 64:96], AG, T.TT[:], mul, ["AG", "TT"], ["Pe"])
-        tt(P[:, 32:64], CH, T.tD[:], mul, ["CH", "tD0", "tD1"], ["Pb"])
-        cp(T.au[:], T.wa[:, 33::2], ["wa"], ["au"])
-        tt(R[:, 32:112], P[:, 0::2], P[:, 1::2], add, ["Pa", "Pb", "Pe", "AG", "CH"], ["R"])
-        tt(R[:, 0:16], R[:, 80:96], T.dE[:], mul, ["R", "dE"], ["Ra"])
-        tt(R[:, 16:32], R[:, 96:112], R[:, 80:96], sub, ["R"], ["Rb"])
-        tt(T.LF[:], R[:, 0:64], T.BASE[:], add, ["R", "Ra", "Rb", "B0", "B1", "B2", "B3"], ["LF"])
-        cp(T.LU[:], T.LF[:], ["LF"], ["LU"])
-
-        S = T["S%d" % (r % 2)]
-        sk = "S%d" % (r % 2)
-        act(T.G2[:], Dm[:].indirect(T.LU[:, 0:16]), AF.Abs, ["Dm%d" % h for h in range(NB)] + ["zb", "zh", "LU"], ["G2"],
-            scale=2.0)
-        tt(T.v2[:], W[:].indirect(T.LU[:, 32:48]), T.G2[:], add, ["Wk%d" % u for u in range(8)] + ["W0", "LU", "G2"], ["v2"])
-        ts(S[:, :, 64:128], T.v2[:], -0.5, 0.5, add, mul, ["v2"], [sk + "z"])
-        cp(T.zn[:], S[:, :, 64:128], [sk + "z"], ["zn"])
-        for b in range(16):
-            mm(bk(4, 256, 272), T.ZU[:, 15 - b:143 - b], T.zn[:, b::16], b == 0, b == 15, ["ZU", "zn"], ["uL"], [4])
-        ts(T.nMi[:], T.QW[:].indirect(T.LU[:, 16:32]), 4095, None, band, None, ["QA", "QB", "Mi", "LU"], ["nMi"])
-        cp(T.ui[:], bk(4, 256, 272), ["uL"], ["ui"], [4])
-        if not last:
-            aff(T.nag[:], R[:, 80:96], -1.0, 1.0, ["R"], ["nag"])
-            cp(S[:, :, 0:64], T.nMi[:], ["nMi"], [sk + "m"])
-            tt(T.c1[:], T.ui[:], T.nag[:], mul, ["ui", "nag"], ["c1"])
-            tt(T.ci[:], T.c1[:], R[:, 64:80], add, ["c1", "R"], ["ci"])
-            ts(T.cn[:], T.ci[:], 1023, None, band, None, ["ci"], ["cn"])
-            cp(S[:, :, 128:132], T.cn[:], ["cn"], [sk + "c"])
-            Ln = T["L%d" % (r + 1)]
-            SK = [sk + "m", sk + "z", sk + "c", sk + "p"]
-
-            def travel(S=S, Ln=Ln, r=r):
-                tr = []
-                for h in range(1, n):
-                    d = dsts[h - 1]
-                    rid, pid, _ = topo.addr(d)
-                    tr.append(RemoteDMATransfer(dst_ids=[DstId(rid=rid, pnc=pid)],
-                                                dma_engine_mask=sum(1 << e for e in eng[d]),
-                                                remote_sem=T.sem["arr%d" % r],
-                                                src=S[:, h, :], dst=Ln[:, (h + 1) % n, :]))
-                g.remote_dma_fused(tr, local_sem=T.sem["snt%d" % r])
-
-            op("g", travel, SK, ["snt%d" % r], sem=("snt%d" % r, sum(len(eng[d]) for d in dsts)))
-            op("g", None, ["snt%d" % r], ["arr"], sem=("arr%d" % r, arrivals))
-            cp(Ln[:, 1, :], S[:, 0, :], SK, ["Lown"])
-
-        ts(T.u15[:], T.ui[:], 15, None, band, None, ["ui"], ["u15"])
-        tt(T.vf[:], T.u15[:], T.c16[:], add, ["u15", "c16"], ["vf"])
-        cp(T.vu[:], T.vf[:], ["vf"], ["vu"])
-        tt(T.sx[:], X[:].indirect(T.vu[:]), T.zn[:], add, ["X", "vu", "zn"], ["sx"])
-        ts(T.sxu[:], T.sx[:], -0.5, 0.5, add, mul, ["sx"], ["sxu"])
-        cp(X[:].indirect(T.vu[:]), T.sxu[:], ["vu", "sxu"], ["X"])
-
-        aff(T.eE[:], T.E[:, 0:16].indirect(T.eu[:]), 1.0, 0.0, ["E", "eu"], ["eE"])
-        aff(bk(4), T.eE[:], 1.0, 0.0, ["eE"], ["p44"], [4])
-        tt(T.Xn[:], bk(4), Mi, mul, ["p44", "Mi"], ["Xn"], [4])
-        tt(T.nb[:], T.LF[:, 48:64], T.i256[:], add, ["LF", "i256"], ["nb"])
-        tt(T.krep[:], T.tab[:].indirect(T.LU[:, 48:64]), T.iF[:], add, ["tab", "LU", "iF"], ["krep"])
-        for a in range(16):
-            for j in range(2):
-                lo, hi = 64 * (a // 4), 16 * (a + 1)
-                c = 16 * j + a
-                act(T.junk[:, 64 * c:64 * c + hi - lo], T.krep[:, lo:hi], AF.Sign, ["krep", "nb", "LF"], ["s%d" % c],
-                    scale=-1.0, bias=T.LF[:, 48 + a:49 + a] if j else T.nb[:, a:a + 1], acc=T.s12[:, c:c + 1])
-        aff(T.old[:], K[:].indirect(T.LU[:, 48:64]), 1.0, 0.0, ["K", "Kd", "LU"], ["old"])
-        aff(T.eA[:], T.E[:, 16:32].indirect(T.au[:]), 1.0, 0.0, ["E", "au"], ["eA"])
-        mm(bk(5), T.Bf[:], T.Xn[:], True, False, ["Bf", "Xn"], ["p45"], [5])
-        mm(bk(5), T.Inf[:], T.old[:], False, True, ["Inf", "old"], ["p45"], [5])
-        tt(T.Y[:], bk(5), T.eA[:], mul, ["p45", "eA"], ["Y"], [5])
-        tt(T.eq[:], T.s12[:, 0:16], T.s12[:, 16:32], ALU.is_equal, ["s%d" % c for c in range(32)], ["eq"])
-        tt(T.of1[:], T.eq[:], R[:, 48:64], mul, ["eq", "R"], ["of1"])
-        tt(T.of2[:], T.of1[:], T.BASE[:, 48:64], add, ["of1", "B3"], ["of2"])
-        cp(T.ofu[:], T.of2[:], ["of2"], ["ofu"])
-        for h in range(NB - 1, -1, -1):
-            tt(K[:].indirect(T.ofu[:, 4 * h:4 * h + 4]), T.old[:, 64 * h:64 * h + 64], T.Y[:, 64 * h:64 * h + 64], add,
-               ["ofu", "old", "Y"], ["K", "Kd"])
-
+            cp(T.cu[:], Lr[:, :, 128:132], ["arr", "Lown"], ["cu"])
+            cp(T.c5[:], Lr[:, :, 132:136], ["arr", "Lown"], ["c5"])
+            cp(T.Mf[:], Lr[:, :, 0:64], ["arr", "Lown"], ks("Mf", blocks), 256)
+        act(T.kcq[:], KW.indirect(T.cu[:]), AF.Identity, ["K", "cu"], ["kcq"], ("g", 256), bias=-2048.0)
+        if r == 0:
+            cp(T.kcu[:], T.kti[:].indirect(T.cu[:]), ["kti", "cu"], ["kcu"], ("g", 256))
+        elif CFG["kcu_a"]:
+            ts(T.kcu[:], T.kcq[:], 2048.0, None, add, None, ["kcq"], ["kcu"], 128)
+        else:
+            cp(T.kcu[:], KW.indirect(T.cu[:]), ["K", "cu"], ["kcu"], ("g", 256))
+        KT, kw = (T.K2, "K2") if last else (K, "K")
         if last:
-            cp(T.nMf[:], T.nMi[:], ["nMi"], ["nMf"])
-            dma("s", T.yz[:], T.zn[:], ["zn"], ["yz"], "oz")
-            dma("s", T.ytx[:], X[:], ["X"], ["ytx"], "ox")
-            dma("s", T.ykt[:], K[:, 0:1024], ["K"], ["ykt"], "ok")
-            dma("s", T.yms[:], T.nMf[:], ["nMf"], ["yms"], "om")
+            dma("s", T.K2[:], K[:], ["K", "Kd"], ["K2"], "k2", 3000)
+        for h in range(2):
+            if not last:
+                aff(T.TT[:, h::2], T.c5[:], 2.0, 2.0 ** 20 + h, ["c5"], ["TT%d" % h])
+            aff(T.TD[:, h::2], T.c5[:], 2.0, SP + 1.0 - h, ["c5"], ["TD%d" % h])
+
+        mord = CFG["mord"][r]
+        units = [u for h in mord for u in (2 * h, 2 * h + 1)]
+        onA = [u for u, x in zip(units, CFG["nb"][r]) if x == "a"]
+        nA = 0
+        for h in mord:
+            us = [u for u in (2 * h, 2 * h + 1) if u not in onA]
+            for u in (2 * h, 2 * h + 1):
+                if u in onA:
+                    b = 4 + nA % 2
+                    nA += 1
+                    pk = ["p%d%s" % (b, x) for x in "abc"]
+                    d = Dm[:, 512 * u:512 * u + 512]
+                    aff(d, X[:].indirect(Lr[:, h, 32 * (u % 2):32 * (u % 2) + 32]), 1.0, 0.0, XK + [lk[h]], ["Dm%d" % u], ("g", 512))
+                    mm(bk(b, 0, 512), [(T.Ib[:], d), (T.Inb[:], zr(u))], ["Ib", "Inb", "Dm%d" % u] + zk(h), pk, b, 1024)
+                    act(T.adM[:, 2 * u:2 * u + 2, :], bk(b, 0, 512), AF.Abs, pk, ["aM%d" % u], 512, [b])
+            if us:
+                m = len(us)
+                d = Dm[:, 512 * us[0]:512 * (us[0] + m)]
+                c0 = 32 * (us[0] % 2)
+                tt(d, X[:].indirect(Lr[:, h, c0:c0 + 32 * m]), zr(us[0], m), sub, XK + [lk[h]] + zk(h), ks("Dm", us), ("g", 512 * m))
+                act(T.adM[:, 2 * us[0]:2 * (us[0] + m), :], d, AF.Abs, ks("Dm", us), ks("aM", us), 512 * m)
+            c0 = home[h][2] + 256 * (4 * h - home[h][0])
+            dma("s", AD[:, c0:c0 + 1024], T.adM[:, 4 * h:4 * h + 4, :], ks("aM", [2 * h, 2 * h + 1]), ["AD%d" % h],
+                "ad%d_%d" % (r, h), 2400)
+        for h in mord:
+            m = CFG["ku"]
+            for u in range(2 * h, 2 * h + 2, m):
+                us = list(range(u, u + m))
+                c0 = home[h][3] + 16 + 256 * (2 * u - home[h][0])
+                d = W[:, c0:c0 + 512 * m]
+                tt(d, X[:].indirect(T.kcu[:, 32 * u:32 * (u + m)]), zr(u, m), sub, XK + ["kcu"] + zk(h), ks("Wk", us), ("g", 512 * m))
+                act(T.adK[:, 2 * u:2 * (u + m), :], d, AF.Abs, ks("Wk", us), ks("aK", us), 512 * m)
+        for t, ad in enumerate((T.adM, T.adK)):
+            for h, m in CFG["sg"][t]:
+                mm(bk(t, 64 * h, 64 * (h + m)), [(T.I4[:], T.oneb[:, 0:64 * m])] * t +
+                   [(T.Z[:, 15 - b:143 - b], ad[:, 4 * h:4 * (h + m), 16 * b:16 * b + 16]) for b in range(16)],
+                   ["I4", "oneb", "Z"] + ks("a" + "MK"[t], range(2 * h, 2 * (h + m))), ks("key%d_" % t, range(h, h + m)), t,
+                   (16 + t) * 64 * m)
+
+        for pn, (a0, a1) in enumerate(parts):
+            hs = list(range(a0 // 4, a1 // 4))
+            us = list(range(a0 // 2, a1 // 2))
+            na, s0, s1 = a1 - a0, 16 * a0, 16 * a1
+            w = s1 - s0
+            sl, la, l2 = slice(s0, s1), slice(a0, a1), slice(2 * a0, 2 * a1)
+            h0, h1 = slice(2 * a0, 2 * a1, 2), slice(2 * a0 + 1, 2 * a1, 2)
+            _p = "_%d" % pn
+
+            def k_(*names):
+                return [x + _p for x in names]
+            zb, ZK, MF = zat(hs[0], len(hs)), ks("zb", hs), ks("Mf", hs)
+            adw = AD[:, home[hs[0]][2]:home[hs[0]][2] + 17 * w]
+            ww = W[:, home[hs[0]][3]:home[hs[0]][3] + 16 + 16 * w]
+
+            q0, q1, hw = a0 // 2, a1 // 2, w // 2
+            for h0_, m in groups(CFG["kg"][0], hs):
+                aff(T.km[:, 0, 2 * h0_:2 * (h0_ + m), :], bk(0, 64 * h0_, 64 * (h0_ + m)), -1.0 / 32, -2040.0,
+                    ks("key0_", range(h0_, h0_ + m)), ks("km", range(h0_, h0_ + m)), 64 * m, [0])
+            for h0_, m in groups(CFG["kg"][1], hs):
+                aff(T.km[:, 1, 2 * h0_:2 * (h0_ + m), :], bk(1, 64 * h0_, 64 * (h0_ + m)), 1.0 / 32, 2039.5,
+                    ks("key1_", range(h0_, h0_ + m)), ks("kk", range(h0_, h0_ + m)), 64 * m, [1])
+            for t in range(2):
+                op("v", lambda t=t, q0=q0, q1=q1: V.transpose(T.tr[:, t, q0:q1, :], T.km[:, t, q0:q1, :]), ks(("km", "kk")[t], hs),
+                   k_("tr%d" % t), ns(w // 2))
+
+            def turned(b, terms, name, j, bias, rd=()):
+                for a2 in range(2):
+                    o = bk(b, s0 + a2 * hw, s0 + (a2 + 1) * hw)
+                    mm(o, [(T.MP[:, 2 * mp + a2, 16 - 16 * (g2 - a2):144 - 16 * (g2 - a2)], T.tr[:, t, q0:q1, 16 * g2:16 * g2 + 16])
+                           for mp, t in terms for g2 in range(2)],
+                       ["MP%d" % (2 * mp + a2) for mp, t in terms] + ["MPp"] + k_(*["tr%d" % t for mp, t in terms]), k_(name + str(a2)),
+                       b, 2 * len(terms) * max(64, hw))
+                for a2 in range(2):
+                    act(T.sg[:, j, q0:q1, 16 * a2:16 * a2 + 16], bk(b, s0 + a2 * hw, s0 + (a2 + 1) * hw), AF.Sign,
+                        k_(name + str(a2)) + list(rd), k_("s%d%d" % (j, a2)), hw, [b], bias=bias)
+
+            turned(2, [(0, 0)], "P2", 0, -0.5)
+            turned(6, [(1, 0), (1, 1)], "P1", 1, -0.5)
+            turned(3, [(2, 1)], "Hs", 2, col[:, 5:6], ["c5_"])
+            fr, p1 = bk(2, 256 + s0, 256 + s1), bk(6, s0, s1)
+            mm(fr, [(T.Ub[:], zb), (T.I37[:], T.oneb[:, sl]), (T.Ib[:], T.kcq[:, sl]), (T.I17[:], T.sg[:, 0, q0:q1, :])],
+               ["Ub", "I37", "oneb", "Ib", "kcq", "I17"] + ZK + k_("s00", "s01"), k_("fr"), 2, 4 * w)
+            aff(T.QW[:, 3 * s0:3 * s1:3], fr, 1.0, 6144.0 - 2.0 ** 17, k_("fr"), k_("QB"), w, [2])
+            mm(p1, [(T.Ib[:], T.kcq[:, sl]), (T.I13[:], T.sg[:, 1, q0:q1, :]), (T.I13[:], T.sg[:, 2, q0:q1, :])],
+               ["Ib", "kcq", "I13"] + k_("s10", "s11", "s20", "s21"), k_("P10", "P11"), 6, 3 * w)
+            aff(T.QW[:, 3 * s0 + 2:3 * s1:3], p1, 1.0, 6144.0 - 16384.0, k_("P10", "P11"), k_("QA"), w, [6])
+
+            e16 = slice(s0 + 15, s1, 16)
+            for t, outs in ((0, ((T.sct, None, T.rs, mul, add, "sct"), (T.scm, None, T.r16, add, mx, "scm"))),
+                            (1, ((T.scs, None, T.rs, mul, add, "scs"), (T.sck, 0, T.r8, add, mx, "sck"), (T.sck, 1, T.rx, add, mn, "scx")))):
+                for h0_, m in groups(CFG["cg"][t], hs):
+                    c0, c1 = 64 * h0_, 64 * (h0_ + m)
+                    for buf, j, mark, o0, o1, name in outs:
+                        scan(buf[:, c0:c1] if j is None else buf[:, j, c0:c1], mark[:, c0:c1], bk(t, c0, c1), o0, o1,
+                             ["rr"] + ks("key%d_" % t, range(h0_, h0_ + m)), ks(name, range(h0_, h0_ + m)), 64 * m, [t])
+                for buf, j, mark, o0, o1, name in outs:
+                    op("n", None, ks(name, hs), k_(name), 0.0)
+            ts(T.ei[:, la], T.scm[:, e16], 15, None, band, None, k_("scm"), k_("ei"))
+            cp(T.eu[:, la], T.ei[:, la], k_("ei"), k_("eu"))
+            tt(T.BASE[:, 0, la], T.cx[:, la], T.ei[:, la], sub, k_("ei") + ["cx"], k_("B0"))
+            act(T.aDT[:, la], T.sct[:, e16], AF.Abs, k_("sct"), k_("aDT"))
+            aff(T.thN[:, la], T.aDT[:, la], -1.0, T.Ac[:, 0:1], k_("aDT") + ["A"], k_("thN"))
+            act(T.tm[:, la], T.thN[:, la], AF.Relu, k_("thN"), k_("tm"), scale=-1.0, bias=-1.0)
+            aff(T.thP[:, la], T.tm[:, la], 1.0, 1.0, k_("tm"), k_("thP"))
+            tt(T.UU[:, h0], T.scs[:, e16], T.thN[:, la], ALU.is_le, k_("scs", "thN"), k_("U0"))
+            tt(T.UU[:, h1], T.scs[:, e16], T.thP[:, la], ALU.is_ge, k_("scs", "thP"), k_("U1"))
+            for h, hh in enumerate((h0, h1)):
+                tt(T.GG[:, hh], T.sck[:, 0, s0 + 7 + 8 * h:s1:16], T.scm[:, e16], ALU.is_gt, k_("sck", "scm"), k_("GG%d" % h))
+            ts(T.wa[:, :, l2], T.sck[:, :, s0 + 7:s1:8], 15, None, band, None, k_("sck", "scx"), k_("wa"))
+            AG, CH, UU = T.AG[:, l2], T.CH[:, l2], T.UU[:, l2]
+            tt(AG, UU, T.GG[:, l2], mul, k_("U0", "U1", "GG0", "GG1"), k_("AG"))
+            tt(T.pK[:, l2], T.pKc[:, l2], T.wa[:, 0, l2], sub, k_("wa") + ["pKc"], k_("pK"))
+            tt(CH, UU, AG, sub, k_("U0", "U1", "AG"), k_("CH"))
+            tt(P[:, 0, l2], AG, T.zp[:, l2], mul, k_("AG") + ["zp"], k_("Pz"))
+            tt(P[:, 1, l2], AG, T.pK[:, l2], mul, k_("AG", "pK"), k_("Pa"))
+            tt(P[:, 2, l2], CH, T.TD[:, l2], mul, k_("CH") + ["TD0", "TD1"], k_("Pb"))
+            tt(P[:, 3, l2], AG, UU, add, k_("AG", "U0", "U1"), k_("Pc"))
+            nr = 4 if last else 5
+            if not last:
+                tt(P[:, 4, l2], AG, T.TT[:, l2], mul, k_("AG") + ["TT0", "TT1"], k_("Pe"))
+            cp(T.au[:, la], T.wa[:, 1, h1], k_("wa"), k_("au"))
+            tt(R[:, 0:nr, la], P[:, 0:nr, h0], P[:, 0:nr, h1], add, k_("Pz", "Pa", "Pb", "Pc", "Pe"), k_("R"), 2 * nr * na)
+            tt(T.LF[:, 0:3, la], R[:, 0:3, la], T.BASE[:, 0:3, la], mx, k_("R", "B0") + ["B1", "B2"], k_("LF"), 6 * na)
+            tt(T.LF[:, 3, la], R[:, 3, la], T.BASE[:, 3, la], add, k_("R") + ["B3"], k_("LF3"))
+            cp(T.LU[:, :, la], T.LF[:, :, la], k_("LF", "LF3"), k_("LU"), 4 * na)
+
+            Ln = None if last else T["L%d" % (r + 1)]
+            own = hs == [0]
+            S, sk = (Ln, "Lo") if own else (T["S%d" % (r % 2)], "S%d" % (r % 2))
+            sb = slice(1, 2) if own else slice(hs[0], hs[-1] + 1)
+            act(T.Hh[:, sl], ww.indirect(T.LU[:, 1, la]), AF.Identity, ks("Wk", us) + ["W0"] + k_("LU"), k_("Hh"), ("g", w),
+                scale=0.5, bias=1023.75)
+            tt(T.zn[:, sl], adw.indirect(T.LU[:, 0, la]), T.Hh[:, sl], add, ks("AD", hs) + ZK + k_("LU", "Hh"), k_("zn"), ("g", w))
+            uL = bk(3, 256 + a0, 256 + a1)
+            mm(uL, [(T.ZU[:, 15 - b:143 - b], T.zn[:, s0 + b:s1:16]) for b in range(16)], ["ZU"] + k_("zn"), k_("uL"), 3, 1024)
+            tt(T.nM[:, sl], T.QW[:, 3 * s0:3 * s1].indirect(T.LU[:, 3, la]), T.Mf[:, sl], mx, k_("QA", "QB", "LU") + ["QC"] + MF,
+               k_("nM"), ("g", w))
+            ts(T.nMi[:, sl], T.nM[:, sl], 4095, None, band, None, k_("nM"), k_("nMi"), w)
+            cp(T.ui[:, la], uL, k_("uL"), k_("ui"), 0, [3])
+            if not last:
+                cb = slice(hs[0], hs[-1] + 1)
+                ts(S[:, sb, 64:128], T.zn[:, sl], -1024.0, None, add, None, k_("zn"), [sk + "z"], w // 2)
+                cp(S[:, sb, 0:64], T.nMi[:, sl], k_("nMi"), [sk + "m"], w)
+                tt(T.ci[:, la], T.ui[:, la], R[:, 4, la], mx, k_("ui", "R"), k_("ci"))
+                ts(T.cn[:, cb, 0, :], T.ci[:, la], 1023, None, band, None, k_("ci"), k_("cn0"))
+                ts(T.cn[:, cb, 1, :], T.ci[:, la], 511, None, band, None, k_("ci"), k_("cn1"))
+                cp(S[:, sb, 128:136], T.cn[:, cb, :, :], k_("cn0", "cn1"), [sk + "c"])
+                SK = [sk + "m", sk + "z", sk + "c"]
+                if own:
+                    op("n", None, SK, ["Lown"], 0.0)
+                else:
+                    def travel(S=S, Ln=Ln, r=r):
+                        tr = []
+                        for h in range(1, n):
+                            d = dsts[h - 1]
+                            rid, pid, _ = topo.addr(d)
+                            tr.append(RemoteDMATransfer(dst_ids=[DstId(rid=rid, pnc=pid)],
+                                                        dma_engine_mask=sum(1 << e for e in eng[d]),
+                                                        remote_sem=T.sem["arr%d" % r],
+                                                        src=S[:, h, :], dst=Ln[:, (h + 1) % n, :]))
+                        g.remote_dma_fused(tr, local_sem=T.sem["snt%d" % r])
+
+                    op("g", travel, SK, ["snt%d" % r], 300.0, d=CFG["rem"] + (2000 if r == 0 else 0),
+                       sem=("snt%d" % r, sum(len(eng[d]) for d in dsts)))
+                    op("x", None, ["snt%d" % r], ["arr"], 0.0, sem=("arr%d" % r, arrivals))
+                    if 0 in hs:
+                        cp(Ln[:, 1, :], S[:, 0, :], SK, ["Lown"], 68)
+
+            xw, XW = X[:, 16 * s0:16 * s1], ks("X", hs)
+            zh = bk(6, 256 + s0, 256 + s1)
+            mm(zh, [(T.Ih[:], T.zn[:, sl])], ["Ih"] + k_("zn"), k_("zh"), 6, w)
+            ts(T.u15[:, la], T.ui[:, la], 15, None, band, None, k_("ui"), k_("u15"))
+            tt(T.vf[:, la], T.u15[:, la], T.cw[:, la], add, k_("u15") + ["cw"], k_("vf"))
+            cp(T.vu[:, la], T.vf[:, la], k_("vf"), k_("vu"))
+            act(T.o2[:, sl], xw.indirect(T.vu[:, la]), AF.Identity, XW + k_("vu"), k_("o2"), ("g", w), scale=0.5, bias=-512.25)
+            tt(T.sx[:, sl], zh, T.o2[:, sl], add, k_("zh", "o2"), k_("sx"), w, [6])
+            cp(xw.indirect(T.vu[:, la]), T.sx[:, sl], k_("vu", "sx"), XW, ("s", w))
+
+            tt(T.Xn[:, sl], T.E[:, 0:16].indirect(T.eu[:, la]), T.Mf[:, sl], mul, ["E"] + k_("eu") + MF, k_("Xn"), ("g", w))
+            aff(T.old[:, sl], K[:].indirect(T.LU[:, 2, la]), 1.0, 0.0, ["K", "Kd"] + k_("LU"), k_("old"), ("g", w))
+            aff(T.eA[:, sl], T.E[:, 16:32].indirect(T.au[:, la]), 1.0, 0.0, ["E"] + k_("au"), k_("eA"), ("g", w))
+            nm = bk(5, s0, s1)
+            mm(nm, [(T.Bf[:], T.Xn[:, sl]), (T.Inf[:], T.old[:, sl])], ["Bf", "Inf"] + k_("Xn", "old"), ["p5a"], 5, 8 * w)
+            tt(T.Y[:, sl], nm, T.eA[:, sl], mul, ["p5a"] + k_("eA"), k_("Y"), w, [5])
+            aff(T.tf[:, la], T.LF[:, 2, la], 1.0, 0.0, k_("LF"), k_("tf"))
+            tt(T.kb[:, la], T.LF[:, 2, la], T.kc[:, la], add, k_("LF") + ["kc"], k_("kb"))
+            mm(bk(7, s0, s1), [(T.I7[:], T.jl[:, sl])] +
+               [(T.DL[:, b, :], T.tf[:, la], T.ps[:, 3584 + s0 + b:3584 + s1:16]) for b in range(16)],
+               ["I7", "jl"] + ks("DL", range(16)) + k_("tf"), k_("rep"), 7, 1024 + w)
+            for a in range(a0, a1):
+                act(T.aD[:, 64 * a:64 * a + 64], bk(7, 64 * (a // 4), 64 * (a // 4) + 64), AF.Abs, k_("rep", "kb"), ["aD%d" % a],
+                    64, [7], scale=-1.0, bias=T.kb[:, a:a + 1])
+            s4 = slice(4 * s0, 4 * s1)
+            scan(T.kp[:, s4], T.r1[:, s4], T.aD[:, s4], mx, mn, ["r1"] + ks("aD", range(a0, a1)), k_("kp"), 2 * w)
+            ts(T.fl[:, la], T.kp[:, 4 * s0 + 63:4 * s1:64], 0.25, None, ALU.is_ge, None, k_("kp"), k_("fl"))
+            tt(T.of1[:, la], T.fl[:, la], R[:, 2, la], mul, k_("fl", "R"), k_("of1"))
+            tt(T.of2[:, la], T.of1[:, la], T.BASE[:, 2, la], mx, k_("of1") + ["B2"], k_("of2"))
+            cp(T.ofu[:, la], T.of2[:, la], k_("of2"), k_("ofu"))
+
+            if last:
+                aff(T.znb[:, sl], T.zn[:, sl], 1.0, -1024.0, k_("zn"), k_("znb"), w)
+                cp(T.nMf[:, sl], T.nMi[:, sl], k_("nMi"), k_("nMf"), w)
+                dma("s", T.yz[:, sl], T.znb[:, sl], k_("znb"), k_("yz"), "oz%d" % pn, 1600)
+                dma("s", T.ytx[:, 16 * s0:16 * s1], xw, XW, k_("ytx"), "ox%d" % pn, 1500 + 12 * w)
+                dma("s", T.yms[:, sl], T.nMf[:, sl], k_("nMf"), k_("yms"), "om%d" % pn, 1700)
+
+        allp = ["_%d" % pn for pn in range(len(parts))]
+        for h in range(NB - 1, -1, -1):
+            _p = [x for x, (a0, a1) in zip(allp, parts) if a0 <= 4 * h < a1][0]
+            tt(KT[:].indirect(T.ofu[:, 4 * h:4 * h + 4]), T.old[:, 64 * h:64 * h + 64], T.Y[:, 64 * h:64 * h + 64], add,
+               ["ofu" + _p, "old" + _p, "Y" + _p], [kw] if last else ["K", "Kd"], ("s", 64))
+        if last:
+            dma("s", T.ykt[:], KT[:, SP:], [kw], ["ykt"], "ok", 3000)
+            op("s", None, ["ykt"] + [x + y for x in ("ytx", "yz", "yms") for y in allp], [], 0.0)
         else:
-            mm(bk(4, 256, 272), T.Bf[:], R[:, 96:112], True, True, ["Bf", "R"], ["uL"], [4])
-            act(T.aj[:], bk(4, 256, 272), AF.Identity, ["uL"], ["aj", "A128"], [4], scale=128.0, acc=T.Ac[:, 0:1])
-            aff(T.Ac[:, 1:2], T.Ac[:, 0:1], 1.0, 64.0, ["A128"], ["A64"])
-            aff(T.Ac[:, 2:3], T.Ac[:, 0:1], 1.0, -1.0, ["A128"], ["Am1"])
-            cp(zb, Ln[:, :, 64:128], ["arr", "Lown"], ["zb"])
-            cp(T.cu[:], Ln[:, :, 128:132], ["arr", "Lown"], ["cu"])
-            if len(FS) == 1:
-                spread(zb, ["zb"], 0, NB, FS[0])
-            else:
-                spread(T.zn[:, 0:64], ["zn"], 1, 1, FS[0])
-                spread(Dm[:, ZB:ZB + 64], ["zb"], 0, 1, FS[1])
-                spread(Dm[:, ZB + 128:ZB + 256], ["zb"], 2, 2, FS[2])
-    op("s", None, ["ytx", "ykt", "yz", "yms"], [])
-    op("g", None, ["snt0", "snt1"], [])
-    emit(g, T, ops[:loads] + [o for o in ordered(ops) if not (o["sem"] and o["sem"][0][:2] == "ld")])
+            mm(bk(3, 288, 320), [(T.Bf[:], T.CH[:])], ["Bf"] + ["CH" + x for x in allp], ["pA"], 3, 256)
+            act(T.aj[:], bk(3, 288, 320), AF.Identity, ["pA"], ["aj", "A"], 200, [3], scale=-256.0, acc=T.Ac[:, 0:1])
+            for h, m, who in CFG["zs"]:
+                src, rd = Ln[:, h:h + m, 64:128], sorted({"Lown" if j == 1 else "arr" for j in range(h, h + m)})
+                cp(zat(h, m), src, rd, ks("zb", range(h, h + m)), 32 * m)
+                spread(h, m, who, src, rd)
+    op("g", None, ["snt0", "snt1"], [], 0.0)
+    alias, out = {}, []
+    for o in ops:
+        o["r"] = [y for x in o["r"] for y in alias.get(x, [x])]
+        if o["e"] == "n":
+            alias[o["w"][0]] = list(o["r"])
+        else:
+            out.append(o)
+    if "order" not in CFG:
+        CFG["order"] = schedule(out)
+    order = [out[j] for j in CFG["order"]]
+    emit(g, T, out[:loads] + [o for o in order if not (o["sem"] and o["sem"][0][:2] == "ld")])

from concourse.bass import DstId, RemoteDMATransfer
from concourse.mybir import AluOpType as ALU, ActivationFunctionType as AF

RO, NB, ROW = 3, 4, 136
SP = 64
BIG = 1.0e6
CFG = {
    "parts": [(0, 16)],
    "nb": ["aavaavav"] * 3,
    "mord": [[0, 1, 2, 3], [1, 2, 3, 0], [1, 2, 3, 0]],
    "zs": [(1, 1, "a" * 8 + "v" * 8), (2, 2, "v" * 16), (0, 1, "g" * 16)],
    "kcu_a": True, "ku": 1,
    "sg": [[(0, 1), (1, 1), (2, 1), (3, 1)]] * 2,
    "kg": [[(0, 4)], [(0, 4)]], "cg": [[(0, 4)], [(0, 4)]],
    "lat": 100.0, "passes": 8, "rem": 2600.0, "gam": 1.3, "f": 1.1,
}


def _sb(n, d):
    return ("sbuf", [128] + (n if isinstance(n, list) else [n]), d)


F, H, I, U, Q = "float32", "bfloat16", "int32", "uint16", "float16"
SCRATCH = {
    "X": _sb(4096, H), "W": _sb(4160, H), "Dm": _sb(4096, H), "zrep": _sb(4096, H),
    "AD": _sb(20 * 256, H), "adM": _sb([16, 256], H), "adK": _sb([16, 256], H),
    "kti": _sb(1024, I), "K": _sb(SP + 1024, F), "K2": _sb(SP + 1024, F), "msi": _sb(256, I), "cpi": _sb(16, I),
    "L0": _sb([NB, ROW], U), "L1": _sb([NB, ROW], U), "L2": _sb([NB, ROW], U),
    "S0": _sb([NB, ROW], U), "S1": _sb([NB, ROW], U),
    "QW": _sb(768, F), "Mf": _sb(256, F), "kcu": _sb(256, U), "kcq": _sb(256, Q), "km": _sb([2, 8, 32], Q), "tr": _sb([2, 8, 32], Q),
    "sg": _sb([3, 8, 32], H), "MP": _sb([6, 160], H), "cx": _sb(16, F), "nM": _sb(256, I), "nMi": _sb(256, I), "nMf": _sb(256, F),
    "Hh": _sb(256, F), "zn": _sb(256, Q), "znb": _sb(256, H), "o2": _sb(256, F), "sx": _sb(256, I),
    "Xn": _sb(256, F), "eA": _sb(256, F), "old": _sb(256, F), "Y": _sb(256, F),
    "aD": _sb(1024, H), "kp": _sb(1024, H), "tf": _sb(16, Q), "kb": _sb(16, F), "fl": _sb(16, F),
    "scm": _sb(256, I), "sct": _sb(256, F), "sck": _sb([2, 256], I), "scs": _sb(256, F),
    "cu": _sb(16, U), "c5": _sb(16, F), "c5i": _sb(16, I), "TT": _sb(32, F), "TD": _sb(32, F),
    "ei": _sb(16, I), "eu": _sb(16, U),
    "aDT": _sb(16, F), "thP": _sb(16, F), "tm": _sb(16, F), "thN": _sb(16, F), "Ac": _sb(4, F), "aj": _sb(32, F),
    "UU": _sb(32, F), "GG": _sb(32, F), "AG": _sb(32, F), "CH": _sb(32, F), "wa": _sb([2, 32], I), "pK": _sb(32, F),
    "P": _sb([5, 32], F), "R": _sb([5, 16], F), "BASE": _sb([4, 16], F), "LF": _sb([4, 16], F), "LU": _sb([4, 16], U),
    "au": _sb(16, U), "ui": _sb(16, I), "u15": _sb(16, I), "vf": _sb(16, F), "vu": _sb(16, U),
    "ci": _sb(16, I), "cn": _sb([NB, 2, 4], I), "of1": _sb(16, F), "of2": _sb(16, F), "ofu": _sb(16, U),
    "ones": _sb(256, F), "oneb": _sb(256, H), "pi": _sb(1, I), "fi": _sb(1, I), "col": _sb(8, F), "If": _sb(128, F),
    "Bt": _sb(128, F), "Bf": _sb(128, F), "Bb": _sb(128, H), "srow": _sb(128, F), "Ht": _sb(128, F), "Hm": _sb(128, H),
    "P2m": _sb(128, H), "t2": _sb(128, F), "Inf": _sb(128, F), "Ih": _sb(128, H), "I13": _sb(128, H), "I17": _sb(128, H),
    "Ib": _sb(128, H), "Inb": _sb(128, H), "I37": _sb(128, Q), "Ub": _sb(128, H), "I7": _sb(128, H),
    "DL": _sb([16, 128], H), "Z": _sb(144, H), "ZU": _sb(144, H), "I4": _sb(128, H), "jl": _sb(256, H),
    "r16": _sb(256, F), "r8": _sb(256, F), "rx": _sb(256, F), "rs": _sb(256, F), "r1": _sb(1024, H),
    "Et": _sb(32, F), "E": _sb(32, F), "i0": _sb(32, F), "iL": _sb(16, F),
    "cw": _sb(16, F), "pKc": _sb(32, F), "zp": _sb(32, F), "kc": _sb(16, F),
    "ps": ("psum", [128, 4096], F),
}
SEMAPHORES = ["v", "a", "p", "g", "ldx", "ldk", "ldm", "ldz0", "ldz1", "ldc", "arr0", "arr1", "snt0", "snt1", "k2",
              "ox0", "ox1", "ok", "om0", "om1", "oz0", "oz1"]
SEMAPHORES += ["ad%d_%d" % (r, h) for r in range(RO) for h in range(NB)]


def engine_split(topo, src, dsts):
    off = [d for d in dsts if topo.chip(d) != topo.chip(src)]
    on = [d for d in dsts if topo.chip(d) == topo.chip(src)]
    used, res = [], {}
    for part in (off, on):
        if not part:
            continue
        free = [e for e in topo.engines(src, part[0]) if e not in used]
        n = 1
        while 2 * n * len(part) <= len(free):
            n *= 2
        for j, d in enumerate(part):
            res[d] = free[j * n:(j + 1) * n]
            used = used + res[d]
    return res


def schedule(ops):
    lat, n = CFG["lat"], len(ops)
    pred, succ = [set() for _ in ops], [[] for _ in ops]
    last_w, readers = {}, {}
    for j, o in enumerate(ops):
        for k in o["r"] + o["w"]:
            if k in last_w:
                pred[j].add(last_w[k])
        for k in o["w"]:
            pred[j].update(readers.get(k, []))
        pred[j].discard(j)
        for k in o["r"]:
            readers.setdefault(k, []).append(j)
        for k in o["w"]:
            last_w[k] = j
            readers[k] = []
        for m in pred[j]:
            succ[m].append(j)

    def gap(m, s):
        return ops[m]["d"] + (0.0 if ops[m]["e"] == "p" and ops[s]["e"] == "p" else lat)

    def place(seq, before, back):
        start, busy = [0.0] * n, {}
        for j in seq:
            o = ops[j]
            s = max([start[m] + ops[m]["t"] + (gap(j, m) if back else gap(m, j)) for m in before[j]] + [o["d"] if back else 0.0])
            t = o["t"]
            taken = [v for v in busy.get(o["e"], []) if v[1] > s]
            for b in o["b"]:
                taken += [(x - lat, y + lat) for x, y, f in busy.get(b, []) if f != o["e"] and y + lat > s]
            for x in sorted(taken):
                if s + t <= x[0]:
                    break
                s = max(s, x[1])
            start[j] = s
            busy.setdefault(o["e"], []).append((s, s + t))
            for b in o["b"]:
                busy.setdefault(b, []).append((s, s + t, o["e"]))
        return start

    way = [0.0] * n
    for j in range(n - 1, -1, -1):
        way[j] = ops[j]["t"] + max([gap(j, s) + way[s] for s in succ[j]] + [ops[j]["d"]])
    seq = sorted(range(n), key=lambda j: (-way[j], j))
    best = None
    for _ in range(CFG["passes"]):
        start = place(seq, pred, False)
        end = max(start[j] + ops[j]["t"] + ops[j]["d"] for j in range(n))
        if best is None or end < best[0]:
            best = (end, start)
        rev = place(sorted(range(n), key=lambda j: (-start[j] - ops[j]["t"], -j)), succ, True)
        seq = sorted(range(n), key=lambda j: (-rev[j] - ops[j]["t"], j))
    CFG["end"] = best[0]
    return sorted(range(n), key=lambda j: (best[1][j], j))


def emit(g, T, ops):
    q = {"v": g.vector, "a": g.scalar, "p": g.tensor, "g": g, "s": g.sync}
    last_w, readers, bank = {}, {}, {}
    clock = {e: {} for e in q}
    done, waits, marked = [], [], set()
    for n, o in enumerate(ops):
        e = o["e"]
        if e == "x":
            waits.append([])
            done.append({o["sem"][0]: n})
            for k in o["w"]:
                last_w[k] = n
                readers[k] = []
            continue
        deps = set()
        for k in o["r"] + o["w"]:
            if k in last_w:
                deps.add(last_w[k])
        for k in o["w"]:
            deps.update(readers.get(k, []))
        for b in o["b"]:
            deps.update(m for f, m in bank.get(b, {}).items() if f != e)
        ws = []
        for m in sorted(deps, reverse=True):
            p = ops[m]
            if p["e"] == "p" and e == "p":
                continue
            key = p["sem"][0] if p["sem"] else p["e"]
            if clock[e].get(key, -1) >= m:
                continue
            ws.append(m)
            marked.add(m)
            for k2, v2 in done[m].items():
                if clock[e].get(k2, -1) < v2:
                    clock[e][k2] = v2
        waits.append(ws)
        d = dict(clock[e])
        d[o["sem"][0] if o["sem"] else e] = n
        done.append(d)
        for k in o["r"]:
            readers.setdefault(k, []).append(n)
        for k in o["w"]:
            last_w[k] = n
            readers[k] = []
        for b in o["b"]:
            bank.setdefault(b, {})[e] = n
    cnt, val = {e: 0 for e in q}, {}
    for n, o in enumerate(ops):
        e = o["e"]
        for m in waits[n]:
            p = ops[m]
            if p["sem"]:
                q[e].wait_ge(T.sem[p["sem"][0]], p["sem"][1])
            else:
                q[e].wait_ge(T.sem[p["e"]], val[m])
        if o["f"] is None:
            continue
        ins = o["f"]()
        if o["sem"]:
            if ins is not None:
                ins.then_inc(T.sem[o["sem"][0]], o["sem"][1])
        elif n in marked:
            cnt[e] += 1
            val[n] = cnt[e]
            ins.then_inc(T.sem[e], 1)


def rank_program(g, core, T, topo):
    rank = T.rank_of(core)
    if rank is None:
        return
    cores = list(T.cores)
    n = len(cores)
    V, A, PE = g.vector, g.scalar, g.tensor
    ops = []

    def op(e, f, r, w, t, b=(), sem=None, d=0.0):
        ops.append({"e": e, "f": f, "r": list(r), "w": list(w), "b": list(b), "sem": sem, "t": t, "d": d})

    def ns(c):
        if isinstance(c, tuple):
            return 55.0 + max(64, c[1]) * (CFG["gam"] if c[0] == "g" else 3.2)
        return CFG["f"] * 0.83 * max(64, c)

    def cp(out, in_, r, w, c=0, b=()):
        op("v", lambda: V.tensor_copy(out, in_), r, w, ns(c), b)

    def tt(out, a, c_, o, r, w, c=0, b=()):
        op("v", lambda: V.tensor_tensor(out, a, c_, o), r, w, ns(c), b)

    def ts(out, a, s1, s2, o0, o1, r, w, c=0, b=()):
        if s2 is None:
            op("v", lambda: V.tensor_scalar(out, a, s1, None, o0), r, w, ns(c), b)
        else:
            op("v", lambda: V.tensor_scalar(out, a, s1, s2, o0, o1), r, w, ns(c), b)

    def ms(out, x, w, c=0):
        op("v", lambda: V.memset(out, x), [], w, ns(c))

    def scan(out, d0, d1, o0, o1, r, w, c, b=()):
        op("v", lambda: V.tensor_tensor_scan(out, d0, d1, 0.0, o0, o1), r, w, ns(c), b)

    def act(out, in_, fn, r, w, c=0, b=(), bias=0.0, scale=1.0, acc=None):
        op("a", lambda: A.activation(out, in_, fn, bias=bias, scale=scale, accum_out=acc), r, w, ns(c), b)

    def aff(out, in_, scale, bias, r, w, c=0, b=()):
        act(out, in_, AF.Identity, r, w, c, b, bias=bias, scale=scale)

    def mm(out, terms, r, w, b, c):
        def run():
            for j, m in enumerate(terms):
                ins = PE.matmul(m[2] if len(m) > 2 else out, m[0], m[1], j == 0, j == len(terms) - 1)
            return ins
        op("p", run, r, w, CFG["f"] * 0.42 * c, [b])

    def iota(out, pat, base, cm, w, c, small=True):
        if small:
            op("g", lambda: g.iota(out, pat, base, cm, allow_small_or_imprecise_dtypes=True), [], w, 140 + 1.8 * c)
        else:
            op("g", lambda: g.iota(out, pat, base, cm), [], w, 140 + 1.8 * c)

    def asel(out, in_, pat, o, fill, base, cm, r, w, c):
        op("g", lambda: g.affine_select(out, in_, pat, o, fill, base, cm), r, w, 185 + 1.8 * c)

    def gcp(out, in_, r, w, c):
        asel(out, in_, [[0, c]], ALU.is_gt, 0.0, 1, 0, r, w, c)

    def dma(e, out, in_, r, w, sem, d):
        qq = g.sync if e == "s" else g.scalar
        op(e, lambda: qq.dma_start(out, in_), r, w, 50.0, sem=(sem, 16), d=d)

    def bk(b, a=0, c=256):
        return T.ps[:, 512 * b + a:512 * b + c]

    def ks(name, hs):
        return ["%s%d" % (name, h) for h in hs]

    W, X, K, Dm, AD = T.W, T.X, T.K, T.Dm, T.AD
    add, sub, mul, mx, mn = ALU.add, ALU.subtract, ALU.mult, ALU.max, ALU.min
    band = ALU.bitwise_and
    ones, col = T.ones, T.col
    blocks = list(range(NB))
    parts = CFG["parts"]
    home = {}
    for j, (a0, a1) in enumerate(sorted(parts)):
        for h in range(a0 // 4, a1 // 4):
            home[h] = (a0, a1, 256 * (a0 + j), 256 * a0 + 16 * j)

    def zat(h, m):
        a0, a1, ad0, _ = home[h]
        c = ad0 + 256 * (a1 - a0) + 64 * h - 16 * a0
        return AD[:, c:c + 64 * m]

    for j, (a0, a1) in enumerate(parts):
        dma("a", zat(a0 // 4, (a1 - a0) // 4), T.z[:, 16 * a0:16 * a1], [], ks("zb", range(a0 // 4, a1 // 4)), "ldz%d" % j, 1700)
    dma("s", T.msi[:], T.ms[:], [], ["msi"], "ldm", 2200)
    dma("a", T.cpi[:], T.cp[:], [], ["cpi"], "ldc", 2400)
    dma("s", X[:], T.tx[:], [], ks("X", blocks), "ldx", 5400)
    dma("s", T.kti[:], T.kt[:], [], ["kti"], "ldk", 7000)
    loads = len(ops)

    ms(ones[:], 1.0, ["ones"], 256)
    ms(T.oneb[:], 1.0, ["oneb"], 128)
    iota(T.pi[:], [[0, 1]], 0, 1, ["pi"], 1, False)
    asel(T.If[:], ones[:, 0:128], [[-1, 128]], ALU.is_equal, 0.0, 0, 1, ["ones"], ["If"], 128)
    asel(T.Bt[:], ones[:, 0:128], [[16, 8], [0, 16]], ALU.is_ge, 0.0, 15, -1, ["ones"], ["Bt"], 128)
    asel(T.Bf[:], T.Bt[:], [[-16, 8], [0, 16]], ALU.is_ge, 0.0, 0, 1, ["Bt"], ["Bf"], 128)
    iota(T.jl[:], [[0, 4], [1, 64]], 0, 0, ["jl"], 256)
    iota(T.i0[:, 0:16], [[16, 16]], 0, 0, ["i0"], 16)
    iota(T.i0[:, 16:32], [[0, 4], [16, 4]], 0, 0, ["i1"], 16)
    iota(T.srow[:], [[0, 8], [-2, 2], [0, 8]], 1, 0, ["srow"], 128)
    iota(T.Et[:, 0:16], [[-1, 16]], 15, 0, ["Et0"], 16)
    iota(T.Et[:, 17:32], [[1, 15]], 0, 0, ["Et1"], 15)
    ms(T.Et[:, 16:17], 15.0, ["Et2"])
    ms(T.MP[:, :, 0:16], 0.0, ["MPp"])
    ms(T.MP[:, :, 144:160], 0.0, ["MPp"])
    ms(T.Z[:], 0.0, ["Z"])
    ms(T.ZU[:], 0.0, ["ZU"])
    ms(T.Ac[:], 0.0, ["A"])
    ms(T.K[:, 0:SP], 0.0, ["Kd"])
    ms(T.BASE[:, 1, :], 0.0, ["B1"])
    ms(T.r1[:], 0.0, ["r1"], 512)
    ms(T.r1[:, 0::64], 1.0, ["r1"])
    ts(T.fi[:], T.pi[:], 15, None, band, None, ["pi"], ["fi"])
    cp(col[:, 0:1], T.fi[:], ["fi"], ["c0"])
    aff(col[:, 1:2], col[:, 0:1], 2.0, 1.0, ["c0"], ["c1_"])
    ts(col[:, 2:3], T.fi[:], 7.5, 2.0, ALU.is_gt, mul, ["fi"], ["c2_"])
    aff(col[:, 3:4], col[:, 0:1], 37.0, 0.0, ["c0"], ["c3_"])
    aff(col[:, 4:5], col[:, 2:3], -1.0, 1.0, ["c2_"], ["c4_"])
    aff(col[:, 5:6], col[:, 2:3], -0.5, 0.5, ["c2_"], ["c5_"])
    for buf, c in ((T.r16, 1.0), (T.r8, 1.0), (T.rx, -1.0), (T.rs, 1.0)):
        aff(buf[:], ones[:], c, 0.0, ["ones"], ["rr"], 256)
    for o_, k_, c in ((T.r16[:, 0::16], 16, -BIG), (T.r8[:, 0::8], 32, -BIG), (T.rx[:, 0::16], 16, BIG), (T.rs[:, 0::16], 16, 0.0), (T.rs[:, 8::16], 16, -1.0)):
        aff(o_, ones[:, 0:k_], c, 0.0, ["ones", "rr"], ["rr"])
    aff(T.QW[:, 1::3], ones[:], -1.0, 0.0, ["ones"], ["QC"], 256)
    for name, c in (("Ib", 1.0), ("Inb", -1.0), ("Inf", -1.0), ("Ih", 0.5), ("I13", 8192.0), ("I17", 2.0 ** 17), ("I7", 1.0 / 128),
                    ("I4", 16.0)):
        aff(T[name][:], T.If[:], c, 0.0, ["If"], [name], 128)
    aff(T.I37[:], T.If[:], col[:, 3:4], 0.0, ["If", "c3_"], ["I37"], 128)
    aff(T.Z[:, 15:128:16], T.Bf[:, 0::16], -32.0, 0.0, ["Bf", "Z"], ["Z"])
    aff(T.ZU[:, 15:128:16], T.Bf[:, 0::16], col[:, 1:2], 0.0, ["Bf", "ZU", "c1_"], ["ZU"])
    aff(T.Ub[:], T.Bf[:], col[:, 1:2], 0.0, ["Bf", "c1_"], ["Ub"], 128)
    aff(T.t2[:], T.Bf[:], -1.0, 0.0, ["Bf"], ["t2"], 128)
    aff(T.Bb[:], T.Bf[:], 1.0, 0.0, ["Bf"], ["Bb"], 128)
    asel(T.P2m[:], T.t2[:], [[-1, 128]], ALU.not_equal, 15.0, 0, 1, ["t2"], ["P2m"], 128)
    aff(T.iL[:], T.i0[:, 0:16], 1.0, col[:, 0:1], ["i0", "c0"], ["iL"])
    aff(T.BASE[:, 2, :], T.i0[:, 16:32], 1.0, col[:, 0:1], ["i1", "c0"], ["B2"])
    aff(T.kc[:], T.BASE[:, 2, :], 1.0 / 128, -0.25, ["B2"], ["kc"])
    aff(T.Ht[:], T.Bf[:], col[:, 4:5], 0.0, ["Bf", "c4_"], ["Ht"], 128)
    for a0, a1 in parts:
        iL, w0 = T.iL[:, a0:a1], home[a0 // 4][3]
        ms(W[:, w0:w0 + 16], 0.0, ["W0"])
        aff(T.cw[:, a0:a1], iL, 16.0, -256.0 * a0, ["iL"], ["cw"])
        aff(T.cx[:, a0:a1], iL, 16.0, 15.0 - 256.0 * a0, ["iL"], ["cx"])
        aff(T.BASE[:, 3, a0:a1], iL, 3.0, -48.0 * a0, ["iL"], ["B3"])
        for h in range(2):
            aff(T.zp[:, 2 * a0 + h:2 * a1:2], iL, 1.0, 256.0 * (a1 - a0) - 16.0 * a0, ["iL"], ["zp"])
            aff(T.pKc[:, 2 * a0 + h:2 * a1:2], iL, 16.0, 8.0 * h + 23.0 - 256.0 * a0, ["iL"], ["pKc"])
    tt(T.Hm[:], T.Ht[:], T.srow[:], mul, ["Ht", "srow"], ["Hm"], 256)
    ts(T.E[:], T.Et[:], col[:, 0:1], None, ALU.is_equal, None, ["Et0", "Et1", "Et2", "c0"], ["E"])
    for j in range(16):
        ts(T.DL[:, j, :], T.Bb[:], T.E[:, 15 - j:16 - j], None, mul, None, ["Bb", "E"], ["DL%d" % j])
    for mp, (src, name) in enumerate(((T.P2m, "P2m"), (T.Ib, "Ib"), (T.Hm, "Hm"))):
        for a2 in range(2):
            asel(T.MP[:, 2 * mp + a2, 16:144], src[:], [[0, 4], [1, 2], [0, 16]], ALU.is_equal, 0.0, -a2, 0, [name],
                 ["MP%d" % (2 * mp + a2)], 128)

    def groups(spec, hs):
        cut = [(max(h, hs[0]), min(h + m, hs[-1] + 1)) for h, m in spec]
        return [(x, y - x) for x, y in cut if y > x]

    dsts = [cores[(rank + h) % n] for h in range(1, n)]
    eng = engine_split(topo, core, dsts)
    arrivals = 0
    for h in range(1, n):
        s = (rank - h) % n
        arrivals += len(engine_split(topo, cores[s], [cores[(s + j) % n] for j in range(1, n)])[core])

    def spread(h, m, who, src=None, r=None):
        hs = list(range(h, h + m))
        for k in range(16):
            o, w = T.zrep[:, 1024 * h + k:1024 * (h + m):16], ks("zr%d_" % k, hs)
            if who[k] == "g":
                gcp(o, zat(h, m), ks("zb", hs), w, 64 * m)
            elif who[k] == "a":
                aff(o, zat(h, m), 1.0, 0.0, ks("zb", hs), w, 64 * m)
            elif src is None:
                cp(o, zat(h, m), ks("zb", hs), w, 32 * m)
            else:
                cp(o, src, r, w, 32 * m)

    def zr(u, m=1):
        return T.zrep[:, 512 * u:512 * (u + m)]

    def zk(h):
        return ["zr%d_%d" % (k, h) for k in range(16)]

    P, R = T.P, T.R
    XK = ks("X", blocks)
    KW = K[:, SP:]

    for r in range(RO):
        last = r == RO - 1
        Lr = T["L%d" % r]
        lk = ["Lm"] * NB if r == 0 else ["arr", "Lown", "arr", "arr"]
        if r == 0:
            for a0, a1 in parts:
                spread(a0 // 4, (a1 - a0) // 4, "v" * 16)
            cp(T.cu[:], T.cpi[:], ["cpi"], ["cu"])
            ts(T.c5i[:], T.cpi[:], 511, None, band, None, ["cpi"], ["c5i"])
            cp(T.c5[:], T.c5i[:], ["c5i"], ["c5"])
            cp(Lr[:, :, 0:64], T.msi[:], ["msi"], ["Lm"], 256)
            gcp(T.Mf[:], T.msi[:], ["msi"], ks("Mf", blocks), 256)
            gcp(KW, T.kti[:], ["kti"], ["K"], 1024)
        else:
            cp(T.cu[:], Lr[:, :, 128:132], ["arr", "Lown"], ["cu"])
            cp(T.c5[:], Lr[:, :, 132:136], ["arr", "Lown"], ["c5"])
            cp(T.Mf[:], Lr[:, :, 0:64], ["arr", "Lown"], ks("Mf", blocks), 256)
        act(T.kcq[:], KW.indirect(T.cu[:]), AF.Identity, ["K", "cu"], ["kcq"], ("g", 256), bias=-2048.0)
        if r == 0:
            cp(T.kcu[:], T.kti[:].indirect(T.cu[:]), ["kti", "cu"], ["kcu"], ("g", 256))
        elif CFG["kcu_a"]:
            ts(T.kcu[:], T.kcq[:], 2048.0, None, add, None, ["kcq"], ["kcu"], 128)
        else:
            cp(T.kcu[:], KW.indirect(T.cu[:]), ["K", "cu"], ["kcu"], ("g", 256))
        KT, kw = (T.K2, "K2") if last else (K, "K")
        if last:
            dma("s", T.K2[:], K[:], ["K", "Kd"], ["K2"], "k2", 3000)
        for h in range(2):
            if not last:
                aff(T.TT[:, h::2], T.c5[:], 2.0, 2.0 ** 20 + h, ["c5"], ["TT%d" % h])
            aff(T.TD[:, h::2], T.c5[:], 2.0, SP + 1.0 - h, ["c5"], ["TD%d" % h])

        mord = CFG["mord"][r]
        units = [u for h in mord for u in (2 * h, 2 * h + 1)]
        onA = [u for u, x in zip(units, CFG["nb"][r]) if x == "a"]
        nA = 0
        for h in mord:
            us = [u for u in (2 * h, 2 * h + 1) if u not in onA]
            for u in (2 * h, 2 * h + 1):
                if u in onA:
                    b = 4 + nA % 2
                    nA += 1
                    pk = ["p%d%s" % (b, x) for x in "abc"]
                    d = Dm[:, 512 * u:512 * u + 512]
                    aff(d, X[:].indirect(Lr[:, h, 32 * (u % 2):32 * (u % 2) + 32]), 1.0, 0.0, XK + [lk[h]], ["Dm%d" % u], ("g", 512))
                    mm(bk(b, 0, 512), [(T.Ib[:], d), (T.Inb[:], zr(u))], ["Ib", "Inb", "Dm%d" % u] + zk(h), pk, b, 1024)
                    act(T.adM[:, 2 * u:2 * u + 2, :], bk(b, 0, 512), AF.Abs, pk, ["aM%d" % u], 512, [b])
            if us:
                m = len(us)
                d = Dm[:, 512 * us[0]:512 * (us[0] + m)]
                c0 = 32 * (us[0] % 2)
                tt(d, X[:].indirect(Lr[:, h, c0:c0 + 32 * m]), zr(us[0], m), sub, XK + [lk[h]] + zk(h), ks("Dm", us), ("g", 512 * m))
                act(T.adM[:, 2 * us[0]:2 * (us[0] + m), :], d, AF.Abs, ks("Dm", us), ks("aM", us), 512 * m)
            c0 = home[h][2] + 256 * (4 * h - home[h][0])
            dma("s", AD[:, c0:c0 + 1024], T.adM[:, 4 * h:4 * h + 4, :], ks("aM", [2 * h, 2 * h + 1]), ["AD%d" % h],
                "ad%d_%d" % (r, h), 2400)
        for h in mord:
            m = CFG["ku"]
            for u in range(2 * h, 2 * h + 2, m):
                us = list(range(u, u + m))
                c0 = home[h][3] + 16 + 256 * (2 * u - home[h][0])
                d = W[:, c0:c0 + 512 * m]
                tt(d, X[:].indirect(T.kcu[:, 32 * u:32 * (u + m)]), zr(u, m), sub, XK + ["kcu"] + zk(h), ks("Wk", us), ("g", 512 * m))
                act(T.adK[:, 2 * u:2 * (u + m), :], d, AF.Abs, ks("Wk", us), ks("aK", us), 512 * m)
        for t, ad in enumerate((T.adM, T.adK)):
            for h, m in CFG["sg"][t]:
                mm(bk(t, 64 * h, 64 * (h + m)), [(T.I4[:], T.oneb[:, 0:64 * m])] * t +
                   [(T.Z[:, 15 - b:143 - b], ad[:, 4 * h:4 * (h + m), 16 * b:16 * b + 16]) for b in range(16)],
                   ["I4", "oneb", "Z"] + ks("a" + "MK"[t], range(2 * h, 2 * (h + m))), ks("key%d_" % t, range(h, h + m)), t,
                   (16 + t) * 64 * m)

        for pn, (a0, a1) in enumerate(parts):
            hs = list(range(a0 // 4, a1 // 4))
            us = list(range(a0 // 2, a1 // 2))
            na, s0, s1 = a1 - a0, 16 * a0, 16 * a1
            w = s1 - s0
            sl, la, l2 = slice(s0, s1), slice(a0, a1), slice(2 * a0, 2 * a1)
            h0, h1 = slice(2 * a0, 2 * a1, 2), slice(2 * a0 + 1, 2 * a1, 2)
            _p = "_%d" % pn

            def k_(*names):
                return [x + _p for x in names]
            zb, ZK, MF = zat(hs[0], len(hs)), ks("zb", hs), ks("Mf", hs)
            adw = AD[:, home[hs[0]][2]:home[hs[0]][2] + 17 * w]
            ww = W[:, home[hs[0]][3]:home[hs[0]][3] + 16 + 16 * w]

            q0, q1, hw = a0 // 2, a1 // 2, w // 2
            for h0_, m in groups(CFG["kg"][0], hs):
                aff(T.km[:, 0, 2 * h0_:2 * (h0_ + m), :], bk(0, 64 * h0_, 64 * (h0_ + m)), -1.0 / 32, -2040.0,
                    ks("key0_", range(h0_, h0_ + m)), ks("km", range(h0_, h0_ + m)), 64 * m, [0])
            for h0_, m in groups(CFG["kg"][1], hs):
                aff(T.km[:, 1, 2 * h0_:2 * (h0_ + m), :], bk(1, 64 * h0_, 64 * (h0_ + m)), 1.0 / 32, 2039.5,
                    ks("key1_", range(h0_, h0_ + m)), ks("kk", range(h0_, h0_ + m)), 64 * m, [1])
            for t in range(2):
                op("v", lambda t=t, q0=q0, q1=q1: V.transpose(T.tr[:, t, q0:q1, :], T.km[:, t, q0:q1, :]), ks(("km", "kk")[t], hs),
                   k_("tr%d" % t), ns(w // 2))

            def turned(b, terms, name, j, bias, rd=()):
                for a2 in range(2):
                    o = bk(b, s0 + a2 * hw, s0 + (a2 + 1) * hw)
                    mm(o, [(T.MP[:, 2 * mp + a2, 16 - 16 * (g2 - a2):144 - 16 * (g2 - a2)], T.tr[:, t, q0:q1, 16 * g2:16 * g2 + 16])
                           for mp, t in terms for g2 in range(2)],
                       ["MP%d" % (2 * mp + a2) for mp, t in terms] + ["MPp"] + k_(*["tr%d" % t for mp, t in terms]), k_(name + str(a2)),
                       b, 2 * len(terms) * max(64, hw))
                for a2 in range(2):
                    act(T.sg[:, j, q0:q1, 16 * a2:16 * a2 + 16], bk(b, s0 + a2 * hw, s0 + (a2 + 1) * hw), AF.Sign,
                        k_(name + str(a2)) + list(rd), k_("s%d%d" % (j, a2)), hw, [b], bias=bias)

            turned(2, [(0, 0)], "P2", 0, -0.5)
            turned(6, [(1, 0), (1, 1)], "P1", 1, -0.5)
            turned(3, [(2, 1)], "Hs", 2, col[:, 5:6], ["c5_"])
            fr, p1 = bk(2, 256 + s0, 256 + s1), bk(6, s0, s1)
            mm(fr, [(T.Ub[:], zb), (T.I37[:], T.oneb[:, sl]), (T.Ib[:], T.kcq[:, sl]), (T.I17[:], T.sg[:, 0, q0:q1, :])],
               ["Ub", "I37", "oneb", "Ib", "kcq", "I17"] + ZK + k_("s00", "s01"), k_("fr"), 2, 4 * w)
            aff(T.QW[:, 3 * s0:3 * s1:3], fr, 1.0, 6144.0 - 2.0 ** 17, k_("fr"), k_("QB"), w, [2])
            mm(p1, [(T.Ib[:], T.kcq[:, sl]), (T.I13[:], T.sg[:, 1, q0:q1, :]), (T.I13[:], T.sg[:, 2, q0:q1, :])],
               ["Ib", "kcq", "I13"] + k_("s10", "s11", "s20", "s21"), k_("P10", "P11"), 6, 3 * w)
            aff(T.QW[:, 3 * s0 + 2:3 * s1:3], p1, 1.0, 6144.0 - 16384.0, k_("P10", "P11"), k_("QA"), w, [6])

            e16 = slice(s0 + 15, s1, 16)
            for t, outs in ((0, ((T.sct, None, T.rs, mul, add, "sct"), (T.scm, None, T.r16, add, mx, "scm"))),
                            (1, ((T.scs, None, T.rs, mul, add, "scs"), (T.sck, 0, T.r8, add, mx, "sck"), (T.sck, 1, T.rx, add, mn, "scx")))):
                for h0_, m in groups(CFG["cg"][t], hs):
                    c0, c1 = 64 * h0_, 64 * (h0_ + m)
                    for buf, j, mark, o0, o1, name in outs:
                        scan(buf[:, c0:c1] if j is None else buf[:, j, c0:c1], mark[:, c0:c1], bk(t, c0, c1), o0, o1,
                             ["rr"] + ks("key%d_" % t, range(h0_, h0_ + m)), ks(name, range(h0_, h0_ + m)), 64 * m, [t])
                for buf, j, mark, o0, o1, name in outs:
                    op("n", None, ks(name, hs), k_(name), 0.0)
            ts(T.ei[:, la], T.scm[:, e16], 15, None, band, None, k_("scm"), k_("ei"))
            cp(T.eu[:, la], T.ei[:, la], k_("ei"), k_("eu"))
            tt(T.BASE[:, 0, la], T.cx[:, la], T.ei[:, la], sub, k_("ei") + ["cx"], k_("B0"))
            act(T.aDT[:, la], T.sct[:, e16], AF.Abs, k_("sct"), k_("aDT"))
            aff(T.thN[:, la], T.aDT[:, la], -1.0, T.Ac[:, 0:1], k_("aDT") + ["A"], k_("thN"))
            act(T.tm[:, la], T.thN[:, la], AF.Relu, k_("thN"), k_("tm"), scale=-1.0, bias=-1.0)
            aff(T.thP[:, la], T.tm[:, la], 1.0, 1.0, k_("tm"), k_("thP"))
            tt(T.UU[:, h0], T.scs[:, e16], T.thN[:, la], ALU.is_le, k_("scs", "thN"), k_("U0"))
            tt(T.UU[:, h1], T.scs[:, e16], T.thP[:, la], ALU.is_ge, k_("scs", "thP"), k_("U1"))
            for h, hh in enumerate((h0, h1)):
                tt(T.GG[:, hh], T.sck[:, 0, s0 + 7 + 8 * h:s1:16], T.scm[:, e16], ALU.is_gt, k_("sck", "scm"), k_("GG%d" % h))
            ts(T.wa[:, :, l2], T.sck[:, :, s0 + 7:s1:8], 15, None, band, None, k_("sck", "scx"), k_("wa"))
            AG, CH, UU = T.AG[:, l2], T.CH[:, l2], T.UU[:, l2]
            tt(AG, UU, T.GG[:, l2], mul, k_("U0", "U1", "GG0", "GG1"), k_("AG"))
            tt(T.pK[:, l2], T.pKc[:, l2], T.wa[:, 0, l2], sub, k_("wa") + ["pKc"], k_("pK"))
            tt(CH, UU, AG, sub, k_("U0", "U1", "AG"), k_("CH"))
            tt(P[:, 0, l2], AG, T.zp[:, l2], mul, k_("AG") + ["zp"], k_("Pz"))
            tt(P[:, 1, l2], AG, T.pK[:, l2], mul, k_("AG", "pK"), k_("Pa"))
            tt(P[:, 2, l2], CH, T.TD[:, l2], mul, k_("CH") + ["TD0", "TD1"], k_("Pb"))
            tt(P[:, 3, l2], AG, UU, add, k_("AG", "U0", "U1"), k_("Pc"))
            nr = 4 if last else 5
            if not last:
                tt(P[:, 4, l2], AG, T.TT[:, l2], mul, k_("AG") + ["TT0", "TT1"], k_("Pe"))
            cp(T.au[:, la], T.wa[:, 1, h1], k_("wa"), k_("au"))
            tt(R[:, 0:nr, la], P[:, 0:nr, h0], P[:, 0:nr, h1], add, k_("Pz", "Pa", "Pb", "Pc", "Pe"), k_("R"), 2 * nr * na)
            tt(T.LF[:, 0:3, la], R[:, 0:3, la], T.BASE[:, 0:3, la], mx, k_("R", "B0") + ["B1", "B2"], k_("LF"), 6 * na)
            tt(T.LF[:, 3, la], R[:, 3, la], T.BASE[:, 3, la], add, k_("R") + ["B3"], k_("LF3"))
            cp(T.LU[:, :, la], T.LF[:, :, la], k_("LF", "LF3"), k_("LU"), 4 * na)

            Ln = None if last else T["L%d" % (r + 1)]
            own = hs == [0]
            S, sk = (Ln, "Lo") if own else (T["S%d" % (r % 2)], "S%d" % (r % 2))
            sb = slice(1, 2) if own else slice(hs[0], hs[-1] + 1)
            act(T.Hh[:, sl], ww.indirect(T.LU[:, 1, la]), AF.Identity, ks("Wk", us) + ["W0"] + k_("LU"), k_("Hh"), ("g", w),
                scale=0.5, bias=1023.75)
            tt(T.zn[:, sl], adw.indirect(T.LU[:, 0, la]), T.Hh[:, sl], add, ks("AD", hs) + ZK + k_("LU", "Hh"), k_("zn"), ("g", w))
            uL = bk(3, 256 + a0, 256 + a1)
            mm(uL, [(T.ZU[:, 15 - b:143 - b], T.zn[:, s0 + b:s1:16]) for b in range(16)], ["ZU"] + k_("zn"), k_("uL"), 3, 1024)
            tt(T.nM[:, sl], T.QW[:, 3 * s0:3 * s1].indirect(T.LU[:, 3, la]), T.Mf[:, sl], mx, k_("QA", "QB", "LU") + ["QC"] + MF,
               k_("nM"), ("g", w))
            ts(T.nMi[:, sl], T.nM[:, sl], 4095, None, band, None, k_("nM"), k_("nMi"), w)
            cp(T.ui[:, la], uL, k_("uL"), k_("ui"), 0, [3])
            if not last:
                cb = slice(hs[0], hs[-1] + 1)
                ts(S[:, sb, 64:128], T.zn[:, sl], -1024.0, None, add, None, k_("zn"), [sk + "z"], w // 2)
                cp(S[:, sb, 0:64], T.nMi[:, sl], k_("nMi"), [sk + "m"], w)
                tt(T.ci[:, la], T.ui[:, la], R[:, 4, la], mx, k_("ui", "R"), k_("ci"))
                ts(T.cn[:, cb, 0, :], T.ci[:, la], 1023, None, band, None, k_("ci"), k_("cn0"))
                ts(T.cn[:, cb, 1, :], T.ci[:, la], 511, None, band, None, k_("ci"), k_("cn1"))
                cp(S[:, sb, 128:136], T.cn[:, cb, :, :], k_("cn0", "cn1"), [sk + "c"])
                SK = [sk + "m", sk + "z", sk + "c"]
                if own:
                    op("n", None, SK, ["Lown"], 0.0)
                else:
                    def travel(S=S, Ln=Ln, r=r):
                        tr = []
                        for h in range(1, n):
                            d = dsts[h - 1]
                            rid, pid, _ = topo.addr(d)
                            tr.append(RemoteDMATransfer(dst_ids=[DstId(rid=rid, pnc=pid)],
                                                        dma_engine_mask=sum(1 << e for e in eng[d]),
                                                        remote_sem=T.sem["arr%d" % r],
                                                        src=S[:, h, :], dst=Ln[:, (h + 1) % n, :]))
                        g.remote_dma_fused(tr, local_sem=T.sem["snt%d" % r])

                    op("g", travel, SK, ["snt%d" % r], 300.0, d=CFG["rem"] + (2000 if r == 0 else 0),
                       sem=("snt%d" % r, sum(len(eng[d]) for d in dsts)))
                    op("x", None, ["snt%d" % r], ["arr"], 0.0, sem=("arr%d" % r, arrivals))
                    if 0 in hs:
                        cp(Ln[:, 1, :], S[:, 0, :], SK, ["Lown"], 68)

            xw, XW = X[:, 16 * s0:16 * s1], ks("X", hs)
            zh = bk(6, 256 + s0, 256 + s1)
            mm(zh, [(T.Ih[:], T.zn[:, sl])], ["Ih"] + k_("zn"), k_("zh"), 6, w)
            ts(T.u15[:, la], T.ui[:, la], 15, None, band, None, k_("ui"), k_("u15"))
            tt(T.vf[:, la], T.u15[:, la], T.cw[:, la], add, k_("u15") + ["cw"], k_("vf"))
            cp(T.vu[:, la], T.vf[:, la], k_("vf"), k_("vu"))
            act(T.o2[:, sl], xw.indirect(T.vu[:, la]), AF.Identity, XW + k_("vu"), k_("o2"), ("g", w), scale=0.5, bias=-512.25)
            tt(T.sx[:, sl], zh, T.o2[:, sl], add, k_("zh", "o2"), k_("sx"), w, [6])
            cp(xw.indirect(T.vu[:, la]), T.sx[:, sl], k_("vu", "sx"), XW, ("s", w))

            tt(T.Xn[:, sl], T.E[:, 0:16].indirect(T.eu[:, la]), T.Mf[:, sl], mul, ["E"] + k_("eu") + MF, k_("Xn"), ("g", w))
            aff(T.old[:, sl], K[:].indirect(T.LU[:, 2, la]), 1.0, 0.0, ["K", "Kd"] + k_("LU"), k_("old"), ("g", w))
            aff(T.eA[:, sl], T.E[:, 16:32].indirect(T.au[:, la]), 1.0, 0.0, ["E"] + k_("au"), k_("eA"), ("g", w))
            nm = bk(5, s0, s1)
            mm(nm, [(T.Bf[:], T.Xn[:, sl]), (T.Inf[:], T.old[:, sl])], ["Bf", "Inf"] + k_("Xn", "old"), ["p5a"], 5, 8 * w)
            tt(T.Y[:, sl], nm, T.eA[:, sl], mul, ["p5a"] + k_("eA"), k_("Y"), w, [5])
            aff(T.tf[:, la], T.LF[:, 2, la], 1.0, 0.0, k_("LF"), k_("tf"))
            tt(T.kb[:, la], T.LF[:, 2, la], T.kc[:, la], add, k_("LF") + ["kc"], k_("kb"))
            mm(bk(7, s0, s1), [(T.I7[:], T.jl[:, sl])] +
               [(T.DL[:, b, :], T.tf[:, la], T.ps[:, 3584 + s0 + b:3584 + s1:16]) for b in range(16)],
               ["I7", "jl"] + ks("DL", range(16)) + k_("tf"), k_("rep"), 7, 1024 + w)
            for a in range(a0, a1):
                act(T.aD[:, 64 * a:64 * a + 64], bk(7, 64 * (a // 4), 64 * (a // 4) + 64), AF.Abs, k_("rep", "kb"), ["aD%d" % a],
                    64, [7], scale=-1.0, bias=T.kb[:, a:a + 1])
            s4 = slice(4 * s0, 4 * s1)
            scan(T.kp[:, s4], T.r1[:, s4], T.aD[:, s4], mx, mn, ["r1"] + ks("aD", range(a0, a1)), k_("kp"), 2 * w)
            ts(T.fl[:, la], T.kp[:, 4 * s0 + 63:4 * s1:64], 0.25, None, ALU.is_ge, None, k_("kp"), k_("fl"))
            tt(T.of1[:, la], T.fl[:, la], R[:, 2, la], mul, k_("fl", "R"), k_("of1"))
            tt(T.of2[:, la], T.of1[:, la], T.BASE[:, 2, la], mx, k_("of1") + ["B2"], k_("of2"))
            cp(T.ofu[:, la], T.of2[:, la], k_("of2"), k_("ofu"))

            if last:
                aff(T.znb[:, sl], T.zn[:, sl], 1.0, -1024.0, k_("zn"), k_("znb"), w)
                cp(T.nMf[:, sl], T.nMi[:, sl], k_("nMi"), k_("nMf"), w)
                dma("s", T.yz[:, sl], T.znb[:, sl], k_("znb"), k_("yz"), "oz%d" % pn, 1600)
                dma("s", T.ytx[:, 16 * s0:16 * s1], xw, XW, k_("ytx"), "ox%d" % pn, 1500 + 12 * w)
                dma("s", T.yms[:, sl], T.nMf[:, sl], k_("nMf"), k_("yms"), "om%d" % pn, 1700)

        allp = ["_%d" % pn for pn in range(len(parts))]
        for h in range(NB - 1, -1, -1):
            _p = [x for x, (a0, a1) in zip(allp, parts) if a0 <= 4 * h < a1][0]
            tt(KT[:].indirect(T.ofu[:, 4 * h:4 * h + 4]), T.old[:, 64 * h:64 * h + 64], T.Y[:, 64 * h:64 * h + 64], add,
               ["ofu" + _p, "old" + _p, "Y" + _p], [kw] if last else ["K", "Kd"], ("s", 64))
        if last:
            dma("s", T.ykt[:], KT[:, SP:], [kw], ["ykt"], "ok", 3000)
            op("s", None, ["ykt"] + [x + y for x in ("ytx", "yz", "yms") for y in allp], [], 0.0)
        else:
            mm(bk(3, 288, 320), [(T.Bf[:], T.CH[:])], ["Bf"] + ["CH" + x for x in allp], ["pA"], 3, 256)
            act(T.aj[:], bk(3, 288, 320), AF.Identity, ["pA"], ["aj", "A"], 200, [3], scale=-256.0, acc=T.Ac[:, 0:1])
            for h, m, who in CFG["zs"]:
                src, rd = Ln[:, h:h + m, 64:128], sorted({"Lown" if j == 1 else "arr" for j in range(h, h + m)})
                cp(zat(h, m), src, rd, ks("zb", range(h, h + m)), 32 * m)
                spread(h, m, who, src, rd)
    op("g", None, ["snt0", "snt1"], [], 0.0)
    alias, out = {}, []
    for o in ops:
        o["r"] = [y for x in o["r"] for y in alias.get(x, [x])]
        if o["e"] == "n":
            alias[o["w"][0]] = list(o["r"])
        else:
            out.append(o)
    if "order" not in CFG:
        CFG["order"] = schedule(out)
    order = [out[j] for j in CFG["order"]]
    emit(g, T, out[:loads] + [o for o in order if not (o["sem"] and o["sem"][0][:2] == "ld")])
